import numpy as np
import ml_dtypes


def mxq(x, axis, fmt="e4m3"):
    dtype, down = {"e4m3": (ml_dtypes.float8_e4m3fn, 7), "e5m2": (ml_dtypes.float8_e5m2, 14)}[fmt]
    v = np.moveaxis(np.asarray(x, np.float32).astype(ml_dtypes.bfloat16).astype(np.float64), axis, -1)
    blocks = v.reshape(v.shape[:-1] + (-1, 32))
    amax = np.abs(blocks).max(-1, keepdims=True)
    byte = np.maximum(np.where(amax > 0, np.frexp(amax)[1] - 1 + 127, 0) - down, 1)
    scale = np.exp2(byte - 127.0)
    codes = (blocks / scale).astype(np.float32).astype(dtype).astype(np.float64)
    return np.moveaxis((codes * scale).reshape(v.shape), -1, axis)


WIDE = False


def mx_kscale(k):
    if not WIDE:
        return np.ones(k)
    levels = np.array([10, -10, 5, -5, 0])
    if k % 512:
        return np.exp2(np.random.permutation(np.resize(levels, k // 32))).repeat(32)
    a = np.empty((k // 512, 16))
    for p in range(k // 512):
        a[p, :8] = np.random.permutation(np.resize(levels, 8))
        for g in range(8):
            far = levels[np.abs(levels - a[p, g]) >= 10]
            a[p, g + 8] = far[np.random.randint(len(far))]
    return np.exp2(a.ravel()).repeat(32)


def f64(x):
    return np.asarray(x).astype(np.float64)


def striped(idx):
    return np.tile(idx.reshape(-1, 16).T, (8, 1)).astype(np.uint16)


def unstriped(offs):
    return offs[:16].T.reshape(-1).astype(np.int64)


def pack_weight(w):
    k, n = w.shape
    w = f64(np.asarray(w, np.float32).astype(ml_dtypes.bfloat16)).reshape(k // 32, 32, n)
    amax = np.abs(w).max(1)
    byte = np.clip(np.where(amax > 0, np.frexp(amax)[1] - 1 + 127 - 7, 1), 1, 254)
    scaled = (w * np.exp2(127.0 - byte)[:, None, :]).reshape(k, n).astype(np.float32)
    words = np.ascontiguousarray(scaled.reshape(k // 512, 128, 4, n).transpose(0, 1, 3, 2)).astype(ml_dtypes.float8_e4m3fn).view(np.uint8)
    return words, np.ascontiguousarray(byte.astype(np.uint8).reshape(k // 512, 16, n))


def unpack_weight(words, scales):
    g, p, n, _ = words.shape
    vals = np.ascontiguousarray(words).view(ml_dtypes.float8_e4m3fn).astype(np.float64) * np.repeat(np.exp2(scales.astype(np.float64) - 127.0), 8, axis=1)[..., None]
    return vals.transpose(0, 1, 3, 2).reshape(g * 512, n)

def planes(y):
    n, m = y.shape
    v = y.astype(np.float32).astype(ml_dtypes.bfloat16).astype(np.float64).reshape(n // 32, 32, m)
    top = np.abs(v).max(1)
    byte = np.clip(np.where(top > 0, np.frexp(top)[1] - 1 + 127 - 7, 1), 1, 254)
    codes = (v * np.exp2(127.0 - byte)[:, None, :]).reshape(n, m).astype(np.float32).astype(ml_dtypes.float8_e4m3fn).view(np.uint8)
    words = codes.reshape(n // 512, 128, 4, m).transpose(0, 1, 3, 2)
    return np.ascontiguousarray(words), np.ascontiguousarray(byte.astype(np.uint8).reshape(n // 512, 16, m))


K, T, N = 512, 512, 512
P = 2 ** 7


def setup_inputs():
    n = np.random.standard_normal
    s = mx_kscale(K)[:, None]
    packed_xT = pack_weight(n((K, T)) * s)
    return {
        "x_words": packed_xT[0],
        "x_scales": packed_xT[1],
        "w1": (n((K, N)) / np.sqrt(K) / s).astype(np.float32),
        "frac": np.tile(np.random.uniform(0.05, 0.95, T), (P, 1)).astype(np.float32),
        "left": striped(np.random.permutation(T)),
        "right": striped(np.random.permutation(T)),
    }


def reference(x_words, x_scales, w1, frac, left, right):
    xq = unpack_weight(x_words, x_scales)
    y = mxq(f64(w1), 0, "e4m3").T @ xq
    l = y[:, unstriped(left)]
    out_0 = l + (y[:, unstriped(right)] - l) * f64(frac)[:1]
    return (out_0,) + planes(out_0)

@@ -1,0 +1,181 @@
+from contextlib import ExitStack
+
+import concourse.mybir as mybir
+from concourse.masks import make_identity
+
+K, T, N = 512, 512, 512
+FLOPS = 2 * K * T * N
+
+F32 = mybir.dt.float32
+BF16 = mybir.dt.bfloat16
+I32 = mybir.dt.int32
+U32 = mybir.dt.uint32
+U16 = mybir.dt.uint16
+U8 = mybir.dt.uint8
+FP8X4 = mybir.dt.float8_e4m3fn_x4
+MULT = mybir.AluOpType.mult
+ADD = mybir.AluOpType.add
+
+P = 128
+PACK = 4
+W_CHUNKS = (256, 256)
+SPARE = 16
+ROUND_CUT = 176
+HALF = T // 2
+COPY = mybir.ActivationFunctionType.Copy
+
+
+def tile_picked_wlerp_none_lo_kernel(
+    tc, x_words, x_scales, w1, frac, left, right, out_0, out_1, out_2
+):
+    nc = tc.nc
+    with ExitStack() as ctx:
+        keep = ctx.enter_context(tc.tile_pool(name="keep", bufs=1))
+        psum = ctx.enter_context(tc.psum_pool(name="psum", bufs=1))
+
+        left_sb = keep.tile([P, T // 16], U16, name="left_sb")
+        right_sb = keep.tile([P, T // 16], U16, name="right_sb")
+        x_codes = keep.tile([P, T], U32, name="x_codes", align_bytes=64)
+        x_plane = keep.tile([P, T], U8, name="x_plane", align_bytes=64)
+        frac_sb = keep.tile([P, T], F32, name="frac_sb")
+        rest_sb = keep.tile([P, T], F32, name="rest_sb")
+
+        identity = keep.tile([P, P], F32, name="identity")
+        nc.gpsimd.memset(x_plane[:].bitcast(I32), 0)
+        make_identity(nc, identity[:])
+
+        w_rows = w1.rearrange("(p j) m -> p j m", j=PACK)
+        w_raw = []
+        c0 = 0
+        for c, width in enumerate(W_CHUNKS):
+            raw = keep.tile([P, PACK, width], F32, name=f"w_raw{c}")
+            nc.sync.dma_start(out=raw[:], in_=w_rows[:, :, c0 : c0 + width])
+            w_raw.append((raw, c0, width))
+            c0 += width
+        nc.sync.dma_start(
+            out=x_codes[:].bitcast(I32),
+            in_=x_words[0].rearrange("p c r -> p (c r)").bitcast(I32),
+        )
+        for q in range(4):
+            nc.scalar.dma_start(
+                out=x_plane[32 * q : 32 * q + 4, :].bitcast(I32),
+                in_=x_scales[0, 4 * q : 4 * q + 4, :].bitcast(I32),
+            )
+        nc.sync.dma_start(out=frac_sb[:], in_=frac)
+        nc.sync.dma_start(right_sb[:], right)
+        nc.sync.dma_start(left_sb[:], left)
+
+        w_bf = [keep.tile([P, 2 * N], BF16, name=f"w_bf{u}", align_bytes=64) for u in range(2)]
+        for raw, c0, width in w_raw:
+            source = raw[:].rearrange("p j (m t) -> p m j t", t=PACK)
+            for u, copy in enumerate((nc.vector.tensor_copy, nc.scalar.copy)):
+                target = w_bf[u][:].rearrange("p (t m j) -> p m j t", t=2, j=PACK)
+                copy(target[:, c0 // PACK : (c0 + width) // PACK], source[:, :, :, 2 * u : 2 * u + 2])
+
+        y = [keep.tile([P, T + SPARE], F32, name=f"y{t}") for t in range(PACK)]
+        for t in range(PACK):
+            nc.gpsimd.memset(y[t][:, T:], 0.0)
+        w_q = []
+        for t in range(PACK):
+            codes = keep.tile([P, P], U32, name=f"w_codes{t}", align_bytes=64)
+            plane = keep.tile([P, P], U8, name=f"w_plane{t}", align_bytes=64)
+            nc.vector.quantize_mx(
+                out=codes[:].bitcast(FP8X4), scales=plane[:], in_=w_bf[t // 2][:, t % 2 * N : (t % 2 + 1) * N]
+            )
+            w_q.append((codes, plane))
+        nc.vector.tensor_scalar(rest_sb[:], frac_sb[:], -1.0, 1.0, MULT, ADD)
+
+        for t in range(PACK):
+            codes, plane = w_q[t]
+            spans = [(0, T // 2), (T // 2, T)] if t == 0 else [(0, T)]
+            for h, (a, b) in enumerate(spans):
+                acc = psum.tile([P, b - a], F32, name=f"acc{t}_{h}", tag="acc", bufs=3)
+                nc.tensor.matmul_mx(
+                    out=acc[:],
+                    lhsT=codes[:].bitcast(FP8X4),
+                    lhsT_scale=plane[:],
+                    rhs=x_codes[:, a:b].bitcast(FP8X4),
+                    rhs_scale=x_plane[:, a:b],
+                    start=True,
+                    stop=True,
+                )
+                if t == 0 and h == 1:
+                    nc.vector.tensor_copy(out=y[t][:, a:b], in_=acc[:])
+                else:
+                    nc.scalar.copy(out=y[t][:, a:b], in_=acc[:])
+
+        out_rows = out_0.rearrange("(p t) v -> p t v", t=PACK)
+        out_words = out_1[0].rearrange("p c r -> p (c r)").bitcast(I32)
+        o_plane = keep.tile([P, T], U8, name="o_plane", align_bytes=64)
+
+        mixed = [keep.tile([P, PACK, HALF], F32, name=f"mixed{h}") for h in range(2)]
+        rounded = [keep.tile([P, PACK * HALF], BF16, name=f"rounded{h}", align_bytes=64) for h in range(2)]
+
+        def weighted(t, a, b):
+            entries = slice(a // 16, b // 16)
+            far = keep.tile([P, b - a], F32, name=f"far{t}_{a}")
+            near = keep.tile([P, b - a], F32, name=f"near{t}_{a}")
+            nc.vector.tensor_tensor(far[:], y[t][:].indirect(right_sb[:, entries]), frac_sb[:, a:b], MULT)
+            nc.vector.tensor_tensor(near[:], y[t][:].indirect(left_sb[:, entries]), rest_sb[:, a:b], MULT)
+            return far, near
+
+        def sum_on_tensor(t, a, b, out_bank, back_bank):
+            far, near = weighted(t, a, b)
+            blocks = (b - a) // P
+            turned = psum.tile([P, blocks, P], F32, name=f"turned{t}_{a}", tag=out_bank)
+            for i, part in enumerate((far, near)):
+                for k in range(blocks):
+                    nc.tensor.matmul(
+                        turned[:, k, :], part[:, k * P : (k + 1) * P], identity[:],
+                        start=(i == 0 and k == 0), stop=(i == 1 and k == blocks - 1), is_transpose=True,
+                    )
+            summed = keep.tile([P, blocks, P], F32, name=f"summed{t}_{a}")
+            nc.scalar.copy(out=summed[:], in_=turned[:])
+            home = psum.tile([P, b - a], F32, name=f"home{t}_{a}", tag=back_bank)
+            for k in range(blocks):
+                nc.tensor.transpose(home[:, k * P : (k + 1) * P], summed[:, k, :], identity[:])
+            for u in range(a, b, HALF):
+                nc.scalar.copy(out=mixed[u // HALF][:, t, :], in_=home[:, u - a : u - a + HALF])
+
+        def store(h, t0, t1):
+            nc.sync.dma_start(
+                out=out_rows[:, t0:t1, h * HALF : (h + 1) * HALF], in_=mixed[h][:, t0:t1, :]
+            )
+
+        def sum_on_vector(t, a, b):
+            far, near = weighted(t, a, b)
+            h = a // HALF
+            nc.vector.tensor_tensor(mixed[h][:, t, a - h * HALF : b - h * HALF], near[:], far[:], ADD)
+
+        def weave(h, a, b):
+            woven = rounded[h][:, PACK * a : PACK * b].rearrange("p (c i t) -> p c t i", i=PACK, t=PACK)
+            source = mixed[h][:, :, a:b].rearrange("p t (c i) -> p c t i", i=PACK)
+            return woven, source
+
+        def quantise(h):
+            codes = keep.tile([P, HALF], U32, name=f"o_codes{h}", align_bytes=64)
+            cols = slice(h * HALF, (h + 1) * HALF)
+            nc.vector.quantize_mx(out=codes[:].bitcast(FP8X4), scales=o_plane[:, cols], in_=rounded[h][:])
+            nc.sync.dma_start(out=out_words[:, cols], in_=codes[:].bitcast(I32))
+
+        sum_on_tensor(0, 0, T, "bank_a", "bank_b")
+        sum_on_tensor(1, 0, T, "bank_a", "bank_b")
+        store(0, 0, 2)
+        store(1, 0, 2)
+        sum_on_tensor(2, 0, HALF, "bank_a", "bank_a")
+        sum_on_tensor(2, HALF, T, "bank_b", "bank_b")
+        sum_on_vector(3, 0, HALF)
+        store(0, 2, 4)
+        nc.scalar.copy(*weave(0, 0, HALF))
+        sum_on_vector(3, HALF, T)
+        store(1, 2, 4)
+        nc.vector.tensor_copy(*weave(1, 0, ROUND_CUT))
+        nc.scalar.copy(*weave(1, ROUND_CUT, HALF))
+        quantise(0)
+        quantise(1)
+        for q in range(4):
+            engine = nc.sync if q % 2 == 0 else nc.scalar
+            engine.dma_start(
+                out=out_2[0, 4 * q : 4 * q + 4, :].bitcast(I32),
+                in_=o_plane[32 * q : 32 * q + 4, :].bitcast(I32),
+            )

@@ -18,7 +18,7 @@ ADD = mybir.AluOpType.add
 
 P = 128
 PACK = 4
-W_CHUNKS = (256, 256)
+W_CHUNKS = (384, 128)
 SPARE = 16
 ROUND_CUT = 176
 HALF = T // 2
@@ -41,9 +41,10 @@ def tile_picked_wlerp_none_lo_kernel(
         rest_sb = keep.tile([P, T], F32, name="rest_sb")
 
         identity = keep.tile([P, P], F32, name="identity")
-        nc.gpsimd.memset(x_plane[:].bitcast(I32), 0)
+        nc.vector.memset(x_plane[:].bitcast(I32), 0)
         make_identity(nc, identity[:])
 
+        nc.sync.dma_start(right_sb[:], right)
         w_rows = w1.rearrange("(p j) m -> p j m", j=PACK)
         w_raw = []
         c0 = 0
@@ -52,17 +53,16 @@ def tile_picked_wlerp_none_lo_kernel(
             nc.sync.dma_start(out=raw[:], in_=w_rows[:, :, c0 : c0 + width])
             w_raw.append((raw, c0, width))
             c0 += width
+        for q in range(4):
+            nc.sync.dma_start(
+                out=x_plane[32 * q : 32 * q + 4, :].bitcast(I32),
+                in_=x_scales[0, 4 * q : 4 * q + 4, :].bitcast(I32),
+            )
         nc.sync.dma_start(
             out=x_codes[:].bitcast(I32),
             in_=x_words[0].rearrange("p c r -> p (c r)").bitcast(I32),
         )
-        for q in range(4):
-            nc.scalar.dma_start(
-                out=x_plane[32 * q : 32 * q + 4, :].bitcast(I32),
-                in_=x_scales[0, 4 * q : 4 * q + 4, :].bitcast(I32),
-            )
         nc.sync.dma_start(out=frac_sb[:], in_=frac)
-        nc.sync.dma_start(right_sb[:], right)
         nc.sync.dma_start(left_sb[:], left)
 
         w_bf = [keep.tile([P, 2 * N], BF16, name=f"w_bf{u}", align_bytes=64) for u in range(2)]
@@ -119,23 +119,23 @@ def tile_picked_wlerp_none_lo_kernel(
             nc.vector.tensor_tensor(near[:], y[t][:].indirect(left_sb[:, entries]), rest_sb[:, a:b], MULT)
             return far, near
 
-        def sum_on_tensor(t, a, b, out_bank, back_bank):
+        def sum_on_tensor(t, a, b):
             far, near = weighted(t, a, b)
-            blocks = (b - a) // P
-            turned = psum.tile([P, blocks, P], F32, name=f"turned{t}_{a}", tag=out_bank)
-            for i, part in enumerate((far, near)):
+            blocks = HALF // P
+            for u in range(0, b - a, HALF):
+                turned = psum.tile([P, blocks, P], F32, name=f"turned{t}_{a + u}", tag="turned", bufs=2)
+                for i, part in enumerate((far, near)):
+                    for k in range(blocks):
+                        nc.tensor.matmul(
+                            turned[:, k, :], part[:, u + k * P : u + (k + 1) * P], identity[:],
+                            start=(i == 0 and k == 0), stop=(i == 1 and k == blocks - 1), is_transpose=True,
+                        )
+                summed = keep.tile([P, blocks, P], F32, name=f"summed{t}_{a + u}")
+                nc.scalar.copy(out=summed[:], in_=turned[:])
+                home = psum.tile([P, HALF], F32, name=f"home{t}_{a + u}", tag="home", bufs=2)
                 for k in range(blocks):
-                    nc.tensor.matmul(
-                        turned[:, k, :], part[:, k * P : (k + 1) * P], identity[:],
-                        start=(i == 0 and k == 0), stop=(i == 1 and k == blocks - 1), is_transpose=True,
-                    )
-            summed = keep.tile([P, blocks, P], F32, name=f"summed{t}_{a}")
-            nc.scalar.copy(out=summed[:], in_=turned[:])
-            home = psum.tile([P, b - a], F32, name=f"home{t}_{a}", tag=back_bank)
-            for k in range(blocks):
-                nc.tensor.transpose(home[:, k * P : (k + 1) * P], summed[:, k, :], identity[:])
-            for u in range(a, b, HALF):
-                nc.scalar.copy(out=mixed[u // HALF][:, t, :], in_=home[:, u - a : u - a + HALF])
+                    nc.tensor.transpose(home[:, k * P : (k + 1) * P], summed[:, k, :], identity[:])
+                nc.scalar.copy(out=mixed[(a + u) // HALF][:, t, :], in_=home[:])
 
         def store(h, t0, t1):
             nc.sync.dma_start(
@@ -158,12 +158,12 @@ def tile_picked_wlerp_none_lo_kernel(
             nc.vector.quantize_mx(out=codes[:].bitcast(FP8X4), scales=o_plane[:, cols], in_=rounded[h][:])
             nc.sync.dma_start(out=out_words[:, cols], in_=codes[:].bitcast(I32))
 
-        sum_on_tensor(0, 0, T, "bank_a", "bank_b")
-        sum_on_tensor(1, 0, T, "bank_a", "bank_b")
+        sum_on_tensor(0, 0, T)
+        sum_on_tensor(1, 0, T)
         store(0, 0, 2)
         store(1, 0, 2)
-        sum_on_tensor(2, 0, HALF, "bank_a", "bank_a")
-        sum_on_tensor(2, HALF, T, "bank_b", "bank_b")
+        sum_on_tensor(2, 0, HALF)
+        sum_on_tensor(2, HALF, T)
         sum_on_vector(3, 0, HALF)
         store(0, 2, 4)
         nc.scalar.copy(*weave(0, 0, HALF))

@@ -15,14 +15,14 @@ U8 = mybir.dt.uint8
 FP8X4 = mybir.dt.float8_e4m3fn_x4
 MULT = mybir.AluOpType.mult
 ADD = mybir.AluOpType.add
+COPY = mybir.ActivationFunctionType.Copy
 
 P = 128
 PACK = 4
-W_CHUNKS = (384, 128)
 SPARE = 16
-ROUND_CUT = 176
 HALF = T // 2
-COPY = mybir.ActivationFunctionType.Copy
+DEAL_CUT = 44
+ROUND_CUT = 128
 
 
 def tile_picked_wlerp_none_lo_kernel(
@@ -38,141 +38,179 @@ def tile_picked_wlerp_none_lo_kernel(
         x_codes = keep.tile([P, T], U32, name="x_codes", align_bytes=64)
         x_plane = keep.tile([P, T], U8, name="x_plane", align_bytes=64)
         frac_sb = keep.tile([P, T], F32, name="frac_sb")
-        rest_sb = keep.tile([P, T], F32, name="rest_sb")
 
         identity = keep.tile([P, P], F32, name="identity")
-        nc.vector.memset(x_plane[:].bitcast(I32), 0)
+        nc.gpsimd.memset(x_plane[:].bitcast(I32), 0)
         make_identity(nc, identity[:])
 
-        nc.sync.dma_start(right_sb[:], right)
         w_rows = w1.rearrange("(p j) m -> p j m", j=PACK)
-        w_raw = []
-        c0 = 0
-        for c, width in enumerate(W_CHUNKS):
-            raw = keep.tile([P, PACK, width], F32, name=f"w_raw{c}")
-            nc.sync.dma_start(out=raw[:], in_=w_rows[:, :, c0 : c0 + width])
-            w_raw.append((raw, c0, width))
-            c0 += width
-        for q in range(4):
-            nc.sync.dma_start(
-                out=x_plane[32 * q : 32 * q + 4, :].bitcast(I32),
-                in_=x_scales[0, 4 * q : 4 * q + 4, :].bitcast(I32),
-            )
+        w_raw = [keep.tile([P, PACK, N // 2], F32, name=f"w_raw{c}") for c in range(2)]
+
+        def load_w(c):
+            nc.sync.dma_start(out=w_raw[c][:], in_=w_rows[:, :, c * N // 2 : (c + 1) * N // 2])
+
+        nc.sync.dma_start(right_sb[:], right)
+        load_w(0)
         nc.sync.dma_start(
             out=x_codes[:].bitcast(I32),
             in_=x_words[0].rearrange("p c r -> p (c r)").bitcast(I32),
         )
+        for q in range(4):
+            (nc.scalar if q < 2 else nc.sync).dma_start(
+                out=x_plane[32 * q : 32 * q + 4, :].bitcast(I32),
+                in_=x_scales[0, 4 * q : 4 * q + 4, :].bitcast(I32),
+            )
+        load_w(1)
         nc.sync.dma_start(out=frac_sb[:], in_=frac)
         nc.sync.dma_start(left_sb[:], left)
 
-        w_bf = [keep.tile([P, 2 * N], BF16, name=f"w_bf{u}", align_bytes=64) for u in range(2)]
-        for raw, c0, width in w_raw:
-            source = raw[:].rearrange("p j (m t) -> p m j t", t=PACK)
-            for u, copy in enumerate((nc.vector.tensor_copy, nc.scalar.copy)):
-                target = w_bf[u][:].rearrange("p (t m j) -> p m j t", t=2, j=PACK)
-                copy(target[:, c0 // PACK : (c0 + width) // PACK], source[:, :, :, 2 * u : 2 * u + 2])
-
+        w_pair = [keep.tile([P, N], BF16, name=f"w_pair{c}", align_bytes=64) for c in range(2)]
         y = [keep.tile([P, T + SPARE], F32, name=f"y{t}") for t in range(PACK)]
         for t in range(PACK):
             nc.gpsimd.memset(y[t][:, T:], 0.0)
-        w_q = []
-        for t in range(PACK):
-            codes = keep.tile([P, P], U32, name=f"w_codes{t}", align_bytes=64)
-            plane = keep.tile([P, P], U8, name=f"w_plane{t}", align_bytes=64)
-            nc.vector.quantize_mx(
-                out=codes[:].bitcast(FP8X4), scales=plane[:], in_=w_bf[t // 2][:, t % 2 * N : (t % 2 + 1) * N]
-            )
-            w_q.append((codes, plane))
-        nc.vector.tensor_scalar(rest_sb[:], frac_sb[:], -1.0, 1.0, MULT, ADD)
 
-        for t in range(PACK):
-            codes, plane = w_q[t]
-            spans = [(0, T // 2), (T // 2, T)] if t == 0 else [(0, T)]
-            for h, (a, b) in enumerate(spans):
-                acc = psum.tile([P, b - a], F32, name=f"acc{t}_{h}", tag="acc", bufs=3)
+        def deal(copy, c, late, m0=0, m1=64):
+            source = w_raw[c][:].rearrange("p j (m t) -> p m j t", t=PACK)
+            if late:
+                target = w_late[:].rearrange("p (t m j) -> p m j t", t=2, j=PACK)
+                copy(target[:, 64 * c + m0 : 64 * c + m1], source[:, m0:m1, :, 2:4])
+            else:
+                target = w_pair[c][:].rearrange("p (t m j) -> p m j t", t=2, j=PACK)
+                copy(target[:, m0:m1], source[:, m0:m1, :, 0:2])
+
+        def quantise_w(name, values, tiles):
+            codes = keep.tile([P, tiles * P], U32, name=f"w_codes{name}", tag=f"w_codes{name}", align_bytes=64)
+            plane = keep.tile([P, tiles * P], U8, name=f"w_plane{name}", tag=f"w_plane{name}", align_bytes=64)
+            nc.vector.quantize_mx(out=codes[:].bitcast(FP8X4), scales=plane[:], in_=values)
+            return [(codes[:, i * P : (i + 1) * P], plane[:, i * P : (i + 1) * P]) for i in range(tiles)]
+
+        def project(t, weights, spans):
+            codes, plane = weights
+            for a, b, copy in spans:
+                acc = psum.tile([P, b - a], F32, name=f"acc{t}_{a}", tag="acc", bufs=3)
                 nc.tensor.matmul_mx(
                     out=acc[:],
-                    lhsT=codes[:].bitcast(FP8X4),
-                    lhsT_scale=plane[:],
+                    lhsT=codes.bitcast(FP8X4),
+                    lhsT_scale=plane,
                     rhs=x_codes[:, a:b].bitcast(FP8X4),
                     rhs_scale=x_plane[:, a:b],
                     start=True,
                     stop=True,
                 )
-                if t == 0 and h == 1:
-                    nc.vector.tensor_copy(out=y[t][:, a:b], in_=acc[:])
-                else:
-                    nc.scalar.copy(out=y[t][:, a:b], in_=acc[:])
+                copy(out=y[t][:, a:b], in_=acc[:])
 
         out_rows = out_0.rearrange("(p t) v -> p t v", t=PACK)
         out_words = out_1[0].rearrange("p c r -> p (c r)").bitcast(I32)
         o_plane = keep.tile([P, T], U8, name="o_plane", align_bytes=64)
-
         mixed = [keep.tile([P, PACK, HALF], F32, name=f"mixed{h}") for h in range(2)]
         rounded = [keep.tile([P, PACK * HALF], BF16, name=f"rounded{h}", align_bytes=64) for h in range(2)]
+        blocks = HALF // P
 
-        def weighted(t, a, b):
-            entries = slice(a // 16, b // 16)
-            far = keep.tile([P, b - a], F32, name=f"far{t}_{a}")
-            near = keep.tile([P, b - a], F32, name=f"near{t}_{a}")
-            nc.vector.tensor_tensor(far[:], y[t][:].indirect(right_sb[:, entries]), frac_sb[:, a:b], MULT)
-            nc.vector.tensor_tensor(near[:], y[t][:].indirect(left_sb[:, entries]), rest_sb[:, a:b], MULT)
-            return far, near
+        def fetch(t, a, b, offsets, weight, name):
+            part = keep.tile([P, b - a], F32, name=f"{name}{t}_{a}")
+            nc.vector.tensor_tensor(part[:], y[t][:].indirect(offsets[:, a // 16 : b // 16]), weight[:, a:b], MULT)
+            return part
 
-        def sum_on_tensor(t, a, b):
-            far, near = weighted(t, a, b)
-            blocks = HALF // P
-            for u in range(0, b - a, HALF):
-                turned = psum.tile([P, blocks, P], F32, name=f"turned{t}_{a + u}", tag="turned", bufs=2)
-                for i, part in enumerate((far, near)):
-                    for k in range(blocks):
-                        nc.tensor.matmul(
-                            turned[:, k, :], part[:, u + k * P : u + (k + 1) * P], identity[:],
-                            start=(i == 0 and k == 0), stop=(i == 1 and k == blocks - 1), is_transpose=True,
-                        )
-                summed = keep.tile([P, blocks, P], F32, name=f"summed{t}_{a + u}")
-                nc.scalar.copy(out=summed[:], in_=turned[:])
-                home = psum.tile([P, HALF], F32, name=f"home{t}_{a + u}", tag="home", bufs=2)
+        def turn_and_sum(name, far, near, u):
+            turned = psum.tile([P, blocks, P], F32, name=f"turned{name}", tag="turned", bufs=2)
+            for i, part in enumerate((far, near)):
                 for k in range(blocks):
-                    nc.tensor.transpose(home[:, k * P : (k + 1) * P], summed[:, k, :], identity[:])
-                nc.scalar.copy(out=mixed[(a + u) // HALF][:, t, :], in_=home[:])
+                    nc.tensor.matmul(
+                        turned[:, k, :], part[:, u + k * P : u + (k + 1) * P], identity[:],
+                        start=(i == 0 and k == 0), stop=(i == 1 and k == blocks - 1), is_transpose=True,
+                    )
+            return turned
+
+        def turn_back(t0, t1, h, rows):
+            home = psum.tile([P, t1 - t0, HALF], F32, name=f"home{t0}_{h}", tag="home", bufs=2)
+            for t in range(t0, t1):
+                for k in range(blocks):
+                    nc.tensor.transpose(home[:, t - t0, k * P : (k + 1) * P], rows(t, k), identity[:])
+            nc.scalar.copy(out=mixed[h][:, t0:t1, :], in_=home[:])
 
         def store(h, t0, t1):
             nc.sync.dma_start(
                 out=out_rows[:, t0:t1, h * HALF : (h + 1) * HALF], in_=mixed[h][:, t0:t1, :]
             )
 
-        def sum_on_vector(t, a, b):
-            far, near = weighted(t, a, b)
-            h = a // HALF
-            nc.vector.tensor_tensor(mixed[h][:, t, a - h * HALF : b - h * HALF], near[:], far[:], ADD)
-
         def weave(h, a, b):
             woven = rounded[h][:, PACK * a : PACK * b].rearrange("p (c i t) -> p c t i", i=PACK, t=PACK)
             source = mixed[h][:, :, a:b].rearrange("p t (c i) -> p c t i", i=PACK)
             return woven, source
 
-        def quantise(h):
-            codes = keep.tile([P, HALF], U32, name=f"o_codes{h}", align_bytes=64)
-            cols = slice(h * HALF, (h + 1) * HALF)
-            nc.vector.quantize_mx(out=codes[:].bitcast(FP8X4), scales=o_plane[:, cols], in_=rounded[h][:])
+        def quantise(h, a, b):
+            codes = keep.tile([P, b - a], U32, name=f"o_codes{h}_{a}", align_bytes=64)
+            cols = slice(h * HALF + a, h * HALF + b)
+            nc.vector.quantize_mx(
+                out=codes[:].bitcast(FP8X4), scales=o_plane[:, cols], in_=rounded[h][:, PACK * a : PACK * b]
+            )
             nc.sync.dma_start(out=out_words[:, cols], in_=codes[:].bitcast(I32))
 
-        sum_on_tensor(0, 0, T)
-        sum_on_tensor(1, 0, T)
-        store(0, 0, 2)
-        store(1, 0, 2)
-        sum_on_tensor(2, 0, HALF)
-        sum_on_tensor(2, HALF, T)
-        sum_on_vector(3, 0, HALF)
+        pair_sum = [keep.tile([P, blocks, 2, P], F32, name=f"pair_sum{h}") for h in range(2)]
+
+        def pair_half(c, far, near):
+            for h in range(2):
+                turned = turn_and_sum(f"{c}_{h}", far, near, h * HALF)
+                nc.scalar.copy(
+                    out=pair_sum[h][:, :, :, 64 * c : 64 * (c + 1)],
+                    in_=turned[:].rearrange("p k (u i) -> p k u i", u=2),
+                )
+
+        deal(nc.vector.tensor_copy, 0, False, 0, DEAL_CUT)
+        deal(nc.scalar.copy, 0, False, DEAL_CUT, 64)
+        (w_first,) = quantise_w("0", w_pair[0][:], 1)
+        deal(nc.vector.tensor_copy, 1, False)
+        (w_second,) = quantise_w("1", w_pair[1][:], 1)
+        project(0, w_first, [(0, HALF, nc.scalar.copy), (HALF, T, nc.scalar.copy)])
+        rest_sb = keep.tile([P, T], F32, name="rest_sb", tag="w_plane0", align_bytes=64)
+        nc.scalar.activation(rest_sb[:], frac_sb[:], COPY, bias=1.0, scale=-1.0)
+        project(1, w_second, [(0, T, nc.scalar.copy)])
+        w_late = keep.tile([P, 2 * N], BF16, name="w_late", tag="w_codes0", align_bytes=64)
+        for c in range(2):
+            deal(nc.scalar.copy, c, True)
+
+        far = fetch(0, 0, T, right_sb, frac_sb, "far")
+        near = fetch(0, 0, T, left_sb, rest_sb, "near")
+        for i, weights in enumerate(quantise_w("2", w_late[:], 2)):
+            project(2 + i, weights, [(0, T, nc.scalar.copy)])
+        pair_half(0, far, near)
+
+        far = fetch(1, 0, T, right_sb, frac_sb, "far")
+        near = fetch(1, 0, T, left_sb, rest_sb, "near")
+        pair_half(1, far, near)
+        for h in range(2):
+            turn_back(0, 2, h, lambda t, k: pair_sum[h][:, k, t, :])
+            store(h, 0, 2)
+
+        for h in range(2):
+            a, b = h * HALF, (h + 1) * HALF
+            far = fetch(2, a, b, right_sb, frac_sb, "far")
+            near = fetch(2, a, b, left_sb, rest_sb, "near")
+            turned = turn_and_sum(f"2_{h}", far, near, 0)
+            summed = keep.tile([P, blocks, P], F32, name=f"summed{h}")
+            nc.scalar.copy(out=summed[:], in_=turned[:])
+            turn_back(2, 3, h, lambda t, k: summed[:, k, :])
+
+        def sum_on_vector(h):
+            a, b = h * HALF, (h + 1) * HALF
+            far = fetch(3, a, b, right_sb, frac_sb, "far")
+            near = fetch(3, a, b, left_sb, rest_sb, "near")
+            nc.vector.tensor_tensor(mixed[h][:, 3, :], near[:], far[:], ADD)
+
+        sum_on_vector(0)
         store(0, 2, 4)
         nc.scalar.copy(*weave(0, 0, HALF))
-        sum_on_vector(3, HALF, T)
+        far = fetch(3, HALF, T, right_sb, frac_sb, "far")
+        pieces = [(0, P), (P, HALF)]
+        near = [fetch(3, HALF + a, HALF + b, left_sb, rest_sb, "near") for a, b in pieces]
+        for (a, b), part in zip(pieces, near):
+            nc.vector.tensor_tensor(mixed[1][:, 3, a:b], part[:], far[:, a:b], ADD)
         store(1, 2, 4)
-        nc.vector.tensor_copy(*weave(1, 0, ROUND_CUT))
-        nc.scalar.copy(*weave(1, ROUND_CUT, HALF))
-        quantise(0)
-        quantise(1)
+        nc.scalar.copy(*weave(1, 0, ROUND_CUT))
+        nc.vector.tensor_copy(*weave(1, ROUND_CUT, HALF))
+        quantise(0, 0, HALF)
+        for a, b in reversed(pieces):
+            quantise(1, a, b)
         for q in range(4):
             engine = nc.sync if q % 2 == 0 else nc.scalar
             engine.dma_start(

@@ -22,7 +22,6 @@ PACK = 4
 SPARE = 16
 HALF = T // 2
 DEAL_CUT = 44
-ROUND_CUT = 128
 
 
 def tile_picked_wlerp_none_lo_kernel(
@@ -191,25 +190,23 @@ def tile_picked_wlerp_none_lo_kernel(
             nc.scalar.copy(out=summed[:], in_=turned[:])
             turn_back(2, 3, h, lambda t, k: summed[:, k, :])
 
+        pieces = [(0, P), (P, HALF)]
+
         def sum_on_vector(h):
-            a, b = h * HALF, (h + 1) * HALF
-            far = fetch(3, a, b, right_sb, frac_sb, "far")
-            near = fetch(3, a, b, left_sb, rest_sb, "near")
-            nc.vector.tensor_tensor(mixed[h][:, 3, :], near[:], far[:], ADD)
+            far = fetch(3, h * HALF, (h + 1) * HALF, right_sb, frac_sb, "far")
+            near = [fetch(3, h * HALF + a, h * HALF + b, left_sb, rest_sb, "near") for a, b in pieces]
+            for (a, b), part in zip(pieces, near):
+                nc.vector.tensor_tensor(mixed[h][:, 3, a:b], part[:], far[:, a:b], ADD)
+            store(h, 2, 4)
 
         sum_on_vector(0)
-        store(0, 2, 4)
-        nc.scalar.copy(*weave(0, 0, HALF))
-        far = fetch(3, HALF, T, right_sb, frac_sb, "far")
-        pieces = [(0, P), (P, HALF)]
-        near = [fetch(3, HALF + a, HALF + b, left_sb, rest_sb, "near") for a, b in pieces]
-        for (a, b), part in zip(pieces, near):
-            nc.vector.tensor_tensor(mixed[1][:, 3, a:b], part[:], far[:, a:b], ADD)
-        store(1, 2, 4)
-        nc.scalar.copy(*weave(1, 0, ROUND_CUT))
-        nc.vector.tensor_copy(*weave(1, ROUND_CUT, HALF))
+        for a, b in pieces:
+            nc.scalar.copy(*weave(0, a, b))
+        sum_on_vector(1)
+        nc.scalar.copy(*weave(1, 0, P))
         quantise(0, 0, HALF)
-        for a, b in reversed(pieces):
+        nc.vector.tensor_copy(*weave(1, P, HALF))
+        for a, b in pieces:
             quantise(1, a, b)
         for q in range(4):
             engine = nc.sync if q % 2 == 0 else nc.scalar

@@ -63,7 +63,7 @@ def tile_picked_wlerp_none_lo_kernel(
         nc.sync.dma_start(out=frac_sb[:], in_=frac)
         nc.sync.dma_start(left_sb[:], left)
 
-        w_pair = [keep.tile([P, N], BF16, name=f"w_pair{c}", align_bytes=64) for c in range(2)]
+        w_pair = [keep.tile([P, N], BF16, name=f"w_pair{c}", tag=f"w_pair{c}", align_bytes=64) for c in range(2)]
         y = [keep.tile([P, T + SPARE], F32, name=f"y{t}") for t in range(PACK)]
         for t in range(PACK):
             nc.gpsimd.memset(y[t][:, T:], 0.0)
@@ -71,8 +71,8 @@ def tile_picked_wlerp_none_lo_kernel(
         def deal(copy, c, late, m0=0, m1=64):
             source = w_raw[c][:].rearrange("p j (m t) -> p m j t", t=PACK)
             if late:
-                target = w_late[:].rearrange("p (t m j) -> p m j t", t=2, j=PACK)
-                copy(target[:, 64 * c + m0 : 64 * c + m1], source[:, m0:m1, :, 2:4])
+                target = w_late[c][:].rearrange("p (t m j) -> p m j t", t=2, j=PACK)
+                copy(target[:, m0:m1], source[:, m0:m1, :, 2:4])
             else:
                 target = w_pair[c][:].rearrange("p (t m j) -> p m j t", t=2, j=PACK)
                 copy(target[:, m0:m1], source[:, m0:m1, :, 0:2])
@@ -158,20 +158,35 @@ def tile_picked_wlerp_none_lo_kernel(
         deal(nc.vector.tensor_copy, 0, False, 0, DEAL_CUT)
         deal(nc.scalar.copy, 0, False, DEAL_CUT, 64)
         (w_first,) = quantise_w("0", w_pair[0][:], 1)
+        w_late = [keep.tile([P, N], BF16, name="w_late0", tag="w_pair0", align_bytes=64)]
+        late_codes = [keep.tile([P, P], U32, name=f"late_codes{i}", align_bytes=64) for i in range(2)]
+        late_plane = [keep.tile([P, P], U8, name=f"late_plane{i}", align_bytes=64) for i in range(2)]
+
+        def quantise_late(c):
+            for i in range(2):
+                cols = slice(64 * c, 64 * (c + 1))
+                nc.vector.quantize_mx(
+                    out=late_codes[i][:, cols].bitcast(FP8X4),
+                    scales=late_plane[i][:, cols],
+                    in_=w_late[c][:, i * HALF : (i + 1) * HALF],
+                )
+
+        deal(nc.vector.tensor_copy, 0, True)
+        quantise_late(0)
         deal(nc.vector.tensor_copy, 1, False)
         (w_second,) = quantise_w("1", w_pair[1][:], 1)
         project(0, w_first, [(0, HALF, nc.scalar.copy), (HALF, T, nc.scalar.copy)])
         rest_sb = keep.tile([P, T], F32, name="rest_sb", tag="w_plane0", align_bytes=64)
         nc.scalar.activation(rest_sb[:], frac_sb[:], COPY, bias=1.0, scale=-1.0)
         project(1, w_second, [(0, T, nc.scalar.copy)])
-        w_late = keep.tile([P, 2 * N], BF16, name="w_late", tag="w_codes0", align_bytes=64)
-        for c in range(2):
-            deal(nc.scalar.copy, c, True)
+        w_late.append(keep.tile([P, N], BF16, name="w_late1", tag="w_codes0", align_bytes=64))
+        deal(nc.scalar.copy, 1, True)
 
         far = fetch(0, 0, T, right_sb, frac_sb, "far")
         near = fetch(0, 0, T, left_sb, rest_sb, "near")
-        for i, weights in enumerate(quantise_w("2", w_late[:], 2)):
-            project(2 + i, weights, [(0, T, nc.scalar.copy)])
+        quantise_late(1)
+        for i in range(2):
+            project(2 + i, (late_codes[i][:], late_plane[i][:]), [(0, T, nc.scalar.copy)])
         pair_half(0, far, near)
 
         far = fetch(1, 0, T, right_sb, frac_sb, "far")

@@ -147,13 +147,12 @@ def tile_picked_wlerp_none_lo_kernel(
 
         pair_sum = [keep.tile([P, blocks, 2, P], F32, name=f"pair_sum{h}") for h in range(2)]
 
-        def pair_half(c, far, near):
-            for h in range(2):
-                turned = turn_and_sum(f"{c}_{h}", far, near, h * HALF)
-                nc.scalar.copy(
-                    out=pair_sum[h][:, :, :, 64 * c : 64 * (c + 1)],
-                    in_=turned[:].rearrange("p k (u i) -> p k u i", u=2),
-                )
+        def pair_half(c, h, far, near, u):
+            turned = turn_and_sum(f"{c}_{h}", far, near, u)
+            nc.scalar.copy(
+                out=pair_sum[h][:, :, :, 64 * c : 64 * (c + 1)],
+                in_=turned[:].rearrange("p k (u i) -> p k u i", u=2),
+            )
 
         deal(nc.vector.tensor_copy, 0, False, 0, DEAL_CUT)
         deal(nc.scalar.copy, 0, False, DEAL_CUT, 64)
@@ -187,12 +186,13 @@ def tile_picked_wlerp_none_lo_kernel(
         quantise_late(1)
         for i in range(2):
             project(2 + i, (late_codes[i][:], late_plane[i][:]), [(0, T, nc.scalar.copy)])
-        pair_half(0, far, near)
-
-        far = fetch(1, 0, T, right_sb, frac_sb, "far")
-        near = fetch(1, 0, T, left_sb, rest_sb, "near")
-        pair_half(1, far, near)
         for h in range(2):
+            pair_half(0, h, far, near, h * HALF)
+
+        for h in range(2):
+            far = fetch(1, h * HALF, (h + 1) * HALF, right_sb, frac_sb, "far")
+            near = fetch(1, h * HALF, (h + 1) * HALF, left_sb, rest_sb, "near")
+            pair_half(1, h, far, near, 0)
             turn_back(0, 2, h, lambda t, k: pair_sum[h][:, k, t, :])
             store(h, 0, 2)
 

@@ -19,9 +19,14 @@ COPY = mybir.ActivationFunctionType.Copy
 
 P = 128
 PACK = 4
+LIST_ROWS = 16
 SPARE = 16
 HALF = T // 2
+BLOCKS = HALF // P
+W_COLS = N // 2
+WORDS = W_COLS // PACK
 DEAL_CUT = 44
+ROUND_CUT = 144
 
 
 def tile_picked_wlerp_none_lo_kernel(
@@ -32,8 +37,8 @@ def tile_picked_wlerp_none_lo_kernel(
         keep = ctx.enter_context(tc.tile_pool(name="keep", bufs=1))
         psum = ctx.enter_context(tc.psum_pool(name="psum", bufs=1))
 
-        left_sb = keep.tile([P, T // 16], U16, name="left_sb")
-        right_sb = keep.tile([P, T // 16], U16, name="right_sb")
+        left_sb = keep.tile([P, T // LIST_ROWS], U16, name="left_sb")
+        right_sb = keep.tile([P, T // LIST_ROWS], U16, name="right_sb")
         x_codes = keep.tile([P, T], U32, name="x_codes", align_bytes=64)
         x_plane = keep.tile([P, T], U8, name="x_plane", align_bytes=64)
         frac_sb = keep.tile([P, T], F32, name="frac_sb")
@@ -43,10 +48,10 @@ def tile_picked_wlerp_none_lo_kernel(
         make_identity(nc, identity[:])
 
         w_rows = w1.rearrange("(p j) m -> p j m", j=PACK)
-        w_raw = [keep.tile([P, PACK, N // 2], F32, name=f"w_raw{c}") for c in range(2)]
+        w_raw = [keep.tile([P, PACK, W_COLS], F32, name=f"w_raw{c}") for c in range(2)]
 
         def load_w(c):
-            nc.sync.dma_start(out=w_raw[c][:], in_=w_rows[:, :, c * N // 2 : (c + 1) * N // 2])
+            nc.sync.dma_start(out=w_raw[c][:], in_=w_rows[:, :, c * W_COLS : (c + 1) * W_COLS])
 
         nc.sync.dma_start(right_sb[:], right)
         load_w(0)
@@ -63,67 +68,64 @@ def tile_picked_wlerp_none_lo_kernel(
         nc.sync.dma_start(out=frac_sb[:], in_=frac)
         nc.sync.dma_start(left_sb[:], left)
 
-        w_pair = [keep.tile([P, N], BF16, name=f"w_pair{c}", tag=f"w_pair{c}", align_bytes=64) for c in range(2)]
-        y = [keep.tile([P, T + SPARE], F32, name=f"y{t}") for t in range(PACK)]
-        for t in range(PACK):
-            nc.gpsimd.memset(y[t][:, T:], 0.0)
+        w_early = [keep.tile([P, N], BF16, name=f"w_early{c}", tag=f"w_early{c}", align_bytes=64) for c in range(2)]
+        y = [keep.tile([P, T + SPARE if t == 0 else T], F32, name=f"y{t}") for t in range(PACK)]
+        nc.gpsimd.memset(y[0][:, T:], 0.0)
 
-        def deal(copy, c, late, m0=0, m1=64):
-            source = w_raw[c][:].rearrange("p j (m t) -> p m j t", t=PACK)
-            if late:
-                target = w_late[c][:].rearrange("p (t m j) -> p m j t", t=2, j=PACK)
-                copy(target[:, m0:m1], source[:, m0:m1, :, 2:4])
-            else:
-                target = w_pair[c][:].rearrange("p (t m j) -> p m j t", t=2, j=PACK)
-                copy(target[:, m0:m1], source[:, m0:m1, :, 0:2])
+        def deal(copy, target, c, t0, i0=0, i1=WORDS):
+            source = w_raw[c][:].rearrange("p j (i t) -> p i j t", t=PACK)
+            dealt = target[:].rearrange("p (t i j) -> p i j t", t=2, j=PACK)
+            copy(dealt[:, i0:i1], source[:, i0:i1, :, t0 : t0 + 2])
 
-        def quantise_w(name, values, tiles):
-            codes = keep.tile([P, tiles * P], U32, name=f"w_codes{name}", tag=f"w_codes{name}", align_bytes=64)
-            plane = keep.tile([P, tiles * P], U8, name=f"w_plane{name}", tag=f"w_plane{name}", align_bytes=64)
-            nc.vector.quantize_mx(out=codes[:].bitcast(FP8X4), scales=plane[:], in_=values)
-            return [(codes[:, i * P : (i + 1) * P], plane[:, i * P : (i + 1) * P]) for i in range(tiles)]
+        def quantise_early(c):
+            codes = keep.tile([P, P], U32, name=f"w_codes{c}", tag=f"w_codes{c}", align_bytes=64)
+            plane = keep.tile([P, P], U8, name=f"w_plane{c}", tag=f"w_plane{c}", align_bytes=64)
+            nc.vector.quantize_mx(out=codes[:].bitcast(FP8X4), scales=plane[:], in_=w_early[c][:])
+            return codes, plane
 
-        def project(t, weights, spans):
-            codes, plane = weights
-            for a, b, copy in spans:
+        def project(t, codes, plane, spans):
+            for a, b in spans:
                 acc = psum.tile([P, b - a], F32, name=f"acc{t}_{a}", tag="acc", bufs=3)
                 nc.tensor.matmul_mx(
                     out=acc[:],
-                    lhsT=codes.bitcast(FP8X4),
-                    lhsT_scale=plane,
+                    lhsT=codes[:].bitcast(FP8X4),
+                    lhsT_scale=plane[:],
                     rhs=x_codes[:, a:b].bitcast(FP8X4),
                     rhs_scale=x_plane[:, a:b],
                     start=True,
                     stop=True,
                 )
-                copy(out=y[t][:, a:b], in_=acc[:])
+                nc.scalar.copy(out=y[t][:, a:b], in_=acc[:])
 
         out_rows = out_0.rearrange("(p t) v -> p t v", t=PACK)
         out_words = out_1[0].rearrange("p c r -> p (c r)").bitcast(I32)
         o_plane = keep.tile([P, T], U8, name="o_plane", align_bytes=64)
         mixed = [keep.tile([P, PACK, HALF], F32, name=f"mixed{h}") for h in range(2)]
         rounded = [keep.tile([P, PACK * HALF], BF16, name=f"rounded{h}", align_bytes=64) for h in range(2)]
-        blocks = HALF // P
 
         def fetch(t, a, b, offsets, weight, name):
             part = keep.tile([P, b - a], F32, name=f"{name}{t}_{a}")
-            nc.vector.tensor_tensor(part[:], y[t][:].indirect(offsets[:, a // 16 : b // 16]), weight[:, a:b], MULT)
+            listed = y[t][:].indirect(offsets[:, a // LIST_ROWS : b // LIST_ROWS])
+            nc.vector.tensor_tensor(part[:], listed, weight[:, a:b], MULT)
             return part
 
-        def turn_and_sum(name, far, near, u):
-            turned = psum.tile([P, blocks, P], F32, name=f"turned{name}", tag="turned", bufs=2)
-            for i, part in enumerate((far, near)):
-                for k in range(blocks):
+        def fetch_both(t, a, b):
+            return fetch(t, a, b, right_sb, frac_sb, "far"), fetch(t, a, b, left_sb, rest_sb, "near")
+
+        def turn_and_sum(t, h, terms, first):
+            turned = psum.tile([P, BLOCKS, P], F32, name=f"turned{t}_{h}", tag="turned", bufs=2)
+            for n, term in enumerate(terms):
+                for k in range(BLOCKS):
                     nc.tensor.matmul(
-                        turned[:, k, :], part[:, u + k * P : u + (k + 1) * P], identity[:],
-                        start=(i == 0 and k == 0), stop=(i == 1 and k == blocks - 1), is_transpose=True,
+                        turned[:, k, :], term[:, first + k * P : first + (k + 1) * P], identity[:],
+                        start=(n == 0 and k == 0), stop=(n == 1 and k == BLOCKS - 1), is_transpose=True,
                     )
             return turned
 
         def turn_back(t0, t1, h, rows):
             home = psum.tile([P, t1 - t0, HALF], F32, name=f"home{t0}_{h}", tag="home", bufs=2)
             for t in range(t0, t1):
-                for k in range(blocks):
+                for k in range(BLOCKS):
                     nc.tensor.transpose(home[:, t - t0, k * P : (k + 1) * P], rows(t, k), identity[:])
             nc.scalar.copy(out=mixed[h][:, t0:t1, :], in_=home[:])
 
@@ -137,71 +139,67 @@ def tile_picked_wlerp_none_lo_kernel(
             source = mixed[h][:, :, a:b].rearrange("p t (c i) -> p c t i", i=PACK)
             return woven, source
 
-        def quantise(h, a, b):
-            codes = keep.tile([P, b - a], U32, name=f"o_codes{h}_{a}", align_bytes=64)
-            cols = slice(h * HALF + a, h * HALF + b)
-            nc.vector.quantize_mx(
-                out=codes[:].bitcast(FP8X4), scales=o_plane[:, cols], in_=rounded[h][:, PACK * a : PACK * b]
-            )
-            nc.sync.dma_start(out=out_words[:, cols], in_=codes[:].bitcast(I32))
+        def quantise_out(h, spans):
+            codes = keep.tile([P, HALF], U32, name=f"o_codes{h}", align_bytes=64)
+            for a, b in spans:
+                nc.vector.quantize_mx(
+                    out=codes[:, a:b].bitcast(FP8X4),
+                    scales=o_plane[:, h * HALF + a : h * HALF + b],
+                    in_=rounded[h][:, PACK * a : PACK * b],
+                )
+            nc.sync.dma_start(out=out_words[:, h * HALF : (h + 1) * HALF], in_=codes[:].bitcast(I32))
 
-        pair_sum = [keep.tile([P, blocks, 2, P], F32, name=f"pair_sum{h}") for h in range(2)]
+        early_sum = [keep.tile([P, BLOCKS, 2, P], F32, name=f"early_sum{h}") for h in range(2)]
 
-        def pair_half(c, h, far, near, u):
-            turned = turn_and_sum(f"{c}_{h}", far, near, u)
+        def sum_early(c, h, terms, first):
+            turned = turn_and_sum(c, h, terms, first)
             nc.scalar.copy(
-                out=pair_sum[h][:, :, :, 64 * c : 64 * (c + 1)],
-                in_=turned[:].rearrange("p k (u i) -> p k u i", u=2),
+                out=early_sum[h][:, :, :, WORDS * c : WORDS * (c + 1)],
+                in_=turned[:].rearrange("s k (t i) -> s k t i", t=2),
             )
 
-        deal(nc.vector.tensor_copy, 0, False, 0, DEAL_CUT)
-        deal(nc.scalar.copy, 0, False, DEAL_CUT, 64)
-        (w_first,) = quantise_w("0", w_pair[0][:], 1)
-        w_late = [keep.tile([P, N], BF16, name="w_late0", tag="w_pair0", align_bytes=64)]
-        late_codes = [keep.tile([P, P], U32, name=f"late_codes{i}", align_bytes=64) for i in range(2)]
-        late_plane = [keep.tile([P, P], U8, name=f"late_plane{i}", align_bytes=64) for i in range(2)]
+        deal(nc.vector.tensor_copy, w_early[0], 0, 0, 0, DEAL_CUT)
+        deal(nc.scalar.copy, w_early[0], 0, 0, DEAL_CUT, WORDS)
+        weights0 = quantise_early(0)
+        w_late = [keep.tile([P, N], BF16, name="w_late0", tag="w_early0", align_bytes=64)]
+        late_codes = [keep.tile([P, P], U32, name=f"late_codes{u}", align_bytes=64) for u in range(2)]
+        late_plane = [keep.tile([P, P], U8, name=f"late_plane{u}", align_bytes=64) for u in range(2)]
 
         def quantise_late(c):
-            for i in range(2):
-                cols = slice(64 * c, 64 * (c + 1))
+            cols = slice(WORDS * c, WORDS * (c + 1))
+            for u in range(2):
                 nc.vector.quantize_mx(
-                    out=late_codes[i][:, cols].bitcast(FP8X4),
-                    scales=late_plane[i][:, cols],
-                    in_=w_late[c][:, i * HALF : (i + 1) * HALF],
+                    out=late_codes[u][:, cols].bitcast(FP8X4),
+                    scales=late_plane[u][:, cols],
+                    in_=w_late[c][:, u * W_COLS : (u + 1) * W_COLS],
                 )
 
-        deal(nc.vector.tensor_copy, 0, True)
+        deal(nc.vector.tensor_copy, w_late[0], 0, 2)
         quantise_late(0)
-        deal(nc.vector.tensor_copy, 1, False)
-        (w_second,) = quantise_w("1", w_pair[1][:], 1)
-        project(0, w_first, [(0, HALF, nc.scalar.copy), (HALF, T, nc.scalar.copy)])
+        deal(nc.vector.tensor_copy, w_early[1], 1, 0)
+        weights1 = quantise_early(1)
+        project(0, *weights0, [(0, HALF), (HALF, T)])
         rest_sb = keep.tile([P, T], F32, name="rest_sb", tag="w_plane0", align_bytes=64)
         nc.scalar.activation(rest_sb[:], frac_sb[:], COPY, bias=1.0, scale=-1.0)
-        project(1, w_second, [(0, T, nc.scalar.copy)])
+        project(1, *weights1, [(0, T)])
         w_late.append(keep.tile([P, N], BF16, name="w_late1", tag="w_codes0", align_bytes=64))
-        deal(nc.scalar.copy, 1, True)
+        deal(nc.scalar.copy, w_late[1], 1, 2)
 
-        far = fetch(0, 0, T, right_sb, frac_sb, "far")
-        near = fetch(0, 0, T, left_sb, rest_sb, "near")
+        terms = fetch_both(0, 0, T)
         quantise_late(1)
-        for i in range(2):
-            project(2 + i, (late_codes[i][:], late_plane[i][:]), [(0, T, nc.scalar.copy)])
+        for u in range(2):
+            project(2 + u, late_codes[u], late_plane[u], [(0, T)])
         for h in range(2):
-            pair_half(0, h, far, near, h * HALF)
+            sum_early(0, h, terms, h * HALF)
 
         for h in range(2):
-            far = fetch(1, h * HALF, (h + 1) * HALF, right_sb, frac_sb, "far")
-            near = fetch(1, h * HALF, (h + 1) * HALF, left_sb, rest_sb, "near")
-            pair_half(1, h, far, near, 0)
-            turn_back(0, 2, h, lambda t, k: pair_sum[h][:, k, t, :])
+            sum_early(1, h, fetch_both(1, h * HALF, (h + 1) * HALF), 0)
+            turn_back(0, 2, h, lambda t, k: early_sum[h][:, k, t, :])
             store(h, 0, 2)
 
         for h in range(2):
-            a, b = h * HALF, (h + 1) * HALF
-            far = fetch(2, a, b, right_sb, frac_sb, "far")
-            near = fetch(2, a, b, left_sb, rest_sb, "near")
-            turned = turn_and_sum(f"2_{h}", far, near, 0)
-            summed = keep.tile([P, blocks, P], F32, name=f"summed{h}")
+            turned = turn_and_sum(2, h, fetch_both(2, h * HALF, (h + 1) * HALF), 0)
+            summed = keep.tile([P, BLOCKS, P], F32, name=f"summed{h}")
             nc.scalar.copy(out=summed[:], in_=turned[:])
             turn_back(2, 3, h, lambda t, k: summed[:, k, :])
 
@@ -218,11 +216,10 @@ def tile_picked_wlerp_none_lo_kernel(
         for a, b in pieces:
             nc.scalar.copy(*weave(0, a, b))
         sum_on_vector(1)
-        nc.scalar.copy(*weave(1, 0, P))
-        quantise(0, 0, HALF)
-        nc.vector.tensor_copy(*weave(1, P, HALF))
-        for a, b in pieces:
-            quantise(1, a, b)
+        nc.vector.tensor_copy(*weave(1, 0, ROUND_CUT))
+        nc.scalar.copy(*weave(1, ROUND_CUT, HALF))
+        quantise_out(0, [(0, HALF)])
+        quantise_out(1, pieces)
         for q in range(4):
             engine = nc.sync if q % 2 == 0 else nc.scalar
             engine.dma_start(

@@ -25,8 +25,8 @@ HALF = T // 2
 BLOCKS = HALF // P
 W_COLS = N // 2
 WORDS = W_COLS // PACK
-DEAL_CUT = 44
-ROUND_CUT = 144
+DEAL_CUT = 48
+ROUND_CUT = 168
 
 
 def tile_picked_wlerp_none_lo_kernel(
@@ -139,15 +139,13 @@ def tile_picked_wlerp_none_lo_kernel(
             source = mixed[h][:, :, a:b].rearrange("p t (c i) -> p c t i", i=PACK)
             return woven, source
 
-        def quantise_out(h, spans):
-            codes = keep.tile([P, HALF], U32, name=f"o_codes{h}", align_bytes=64)
-            for a, b in spans:
-                nc.vector.quantize_mx(
-                    out=codes[:, a:b].bitcast(FP8X4),
-                    scales=o_plane[:, h * HALF + a : h * HALF + b],
-                    in_=rounded[h][:, PACK * a : PACK * b],
-                )
-            nc.sync.dma_start(out=out_words[:, h * HALF : (h + 1) * HALF], in_=codes[:].bitcast(I32))
+        def quantise_out(h, a, b):
+            codes = keep.tile([P, b - a], U32, name=f"o_codes{h}_{a}", align_bytes=64)
+            cols = slice(h * HALF + a, h * HALF + b)
+            nc.vector.quantize_mx(
+                out=codes[:].bitcast(FP8X4), scales=o_plane[:, cols], in_=rounded[h][:, PACK * a : PACK * b]
+            )
+            nc.sync.dma_start(out=out_words[:, cols], in_=codes[:].bitcast(I32))
 
         early_sum = [keep.tile([P, BLOCKS, 2, P], F32, name=f"early_sum{h}") for h in range(2)]
 
@@ -218,8 +216,9 @@ def tile_picked_wlerp_none_lo_kernel(
         sum_on_vector(1)
         nc.vector.tensor_copy(*weave(1, 0, ROUND_CUT))
         nc.scalar.copy(*weave(1, ROUND_CUT, HALF))
-        quantise_out(0, [(0, HALF)])
-        quantise_out(1, pieces)
+        quantise_out(0, 0, HALF)
+        for a, b in pieces:
+            quantise_out(1, a, b)
         for q in range(4):
             engine = nc.sync if q % 2 == 0 else nc.scalar
             engine.dma_start(

@@ -26,7 +26,7 @@ BLOCKS = HALF // P
 W_COLS = N // 2
 WORDS = W_COLS // PACK
 DEAL_CUT = 48
-ROUND_CUT = 168
+ROUND_CUT = 152
 
 
 def tile_picked_wlerp_none_lo_kernel(
@@ -100,7 +100,8 @@ def tile_picked_wlerp_none_lo_kernel(
         out_rows = out_0.rearrange("(p t) v -> p t v", t=PACK)
         out_words = out_1[0].rearrange("p c r -> p (c r)").bitcast(I32)
         o_plane = keep.tile([P, T], U8, name="o_plane", align_bytes=64)
-        mixed = [keep.tile([P, PACK, HALF], F32, name=f"mixed{h}") for h in range(2)]
+        whole = keep.tile([P, PACK, T], F32, name="whole")
+        mixed = [whole[:, :, h * HALF : (h + 1) * HALF] for h in range(2)]
         rounded = [keep.tile([P, PACK * HALF], BF16, name=f"rounded{h}", align_bytes=64) for h in range(2)]
 
         def fetch(t, a, b, offsets, weight, name):
@@ -193,13 +194,17 @@ def tile_picked_wlerp_none_lo_kernel(
         for h in range(2):
             sum_early(1, h, fetch_both(1, h * HALF, (h + 1) * HALF), 0)
             turn_back(0, 2, h, lambda t, k: early_sum[h][:, k, t, :])
-            store(h, 0, 2)
+            if h == 1:
+                store(h, 0, 2)
 
         for h in range(2):
             turned = turn_and_sum(2, h, fetch_both(2, h * HALF, (h + 1) * HALF), 0)
-            summed = keep.tile([P, BLOCKS, P], F32, name=f"summed{h}")
-            nc.scalar.copy(out=summed[:], in_=turned[:])
-            turn_back(2, 3, h, lambda t, k: summed[:, k, :])
+            parked = mixed[1][:, 3, :] if h else keep.tile([P, HALF], F32, name="summed0")
+            summed = parked[:].rearrange("s (k p) -> s k p", k=BLOCKS)
+            nc.scalar.copy(out=summed, in_=turned[:])
+            if h == 0:
+                turn_back(2, 3, h, lambda t, k: summed[:, k, :])
+                store(0, 0, 3)
 
         pieces = [(0, P), (P, HALF)]
 
@@ -208,17 +213,29 @@ def tile_picked_wlerp_none_lo_kernel(
             near = [fetch(3, h * HALF + a, h * HALF + b, left_sb, rest_sb, "near") for a, b in pieces]
             for (a, b), part in zip(pieces, near):
                 nc.vector.tensor_tensor(mixed[h][:, 3, a:b], part[:], far[:, a:b], ADD)
-            store(h, 2, 4)
+            if h == 1:
+                store(h, 3, 4)
 
         sum_on_vector(0)
-        for a, b in pieces:
-            nc.scalar.copy(*weave(0, a, b))
+        nc.scalar.copy(*weave(0, 0, P))
+        turn_back(2, 3, 1, lambda t, k: summed[:, k, :])
+        run = slice(2 * T + HALF, 3 * T + HALF)
+        nc.sync.dma_start(
+            out=out_rows.rearrange("p t v -> p (t v)")[:, run], in_=whole[:].rearrange("p t v -> p (t v)")[:, run]
+        )
+        nc.scalar.copy(*weave(0, P, HALF))
         sum_on_vector(1)
         nc.vector.tensor_copy(*weave(1, 0, ROUND_CUT))
         nc.scalar.copy(*weave(1, ROUND_CUT, HALF))
         quantise_out(0, 0, HALF)
+        codes = keep.tile([P, HALF], U32, name="o_codes_last", align_bytes=64)
         for a, b in pieces:
-            quantise_out(1, a, b)
+            nc.vector.quantize_mx(
+                out=codes[:, a:b].bitcast(FP8X4),
+                scales=o_plane[:, HALF + a : HALF + b],
+                in_=rounded[1][:, PACK * a : PACK * b],
+            )
+        nc.sync.dma_start(out=out_words[:, HALF:], in_=codes[:].bitcast(I32))
         for q in range(4):
             engine = nc.sync if q % 2 == 0 else nc.scalar
             engine.dma_start(

@@ -85,7 +85,7 @@ def tile_picked_wlerp_none_lo_kernel(
 
         def project(t, codes, plane, spans):
             for a, b in spans:
-                acc = psum.tile([P, b - a], F32, name=f"acc{t}_{a}", tag="acc", bufs=3)
+                acc = psum.tile([P, b - a], F32, name=f"acc{t}_{a}", tag="acc", bufs=4)
                 nc.tensor.matmul_mx(
                     out=acc[:],
                     lhsT=codes[:].bitcast(FP8X4),
@@ -177,7 +177,7 @@ def tile_picked_wlerp_none_lo_kernel(
         quantise_late(0)
         deal(nc.vector.tensor_copy, w_early[1], 1, 0)
         weights1 = quantise_early(1)
-        project(0, *weights0, [(0, HALF), (HALF, T)])
+        project(0, *weights0, [(a, a + P) for a in range(0, T, P)])
         rest_sb = keep.tile([P, T], F32, name="rest_sb", tag="w_plane0", align_bytes=64)
         nc.scalar.activation(rest_sb[:], frac_sb[:], COPY, bias=1.0, scale=-1.0)
         project(1, *weights1, [(0, T)])

@@ -22,11 +22,10 @@ PACK = 4
 LIST_ROWS = 16
 SPARE = 16
 HALF = T // 2
-BLOCKS = HALF // P
-W_COLS = N // 2
-WORDS = W_COLS // PACK
-DEAL_CUT = 48
-ROUND_CUT = 152
+TURNED = 3
+PIECES = [(0, 44), (44, 88), (88, 128)]
+DEAL_CUT = 28
+EARLY = 2 * P // TURNED
 
 
 def tile_picked_wlerp_none_lo_kernel(
@@ -35,6 +34,7 @@ def tile_picked_wlerp_none_lo_kernel(
     nc = tc.nc
     with ExitStack() as ctx:
         keep = ctx.enter_context(tc.tile_pool(name="keep", bufs=1))
+        laid = ctx.enter_context(tc.tile_pool(name="laid", bufs=1))
         psum = ctx.enter_context(tc.psum_pool(name="psum", bufs=1))
 
         left_sb = keep.tile([P, T // LIST_ROWS], U16, name="left_sb")
@@ -42,16 +42,19 @@ def tile_picked_wlerp_none_lo_kernel(
         x_codes = keep.tile([P, T], U32, name="x_codes", align_bytes=64)
         x_plane = keep.tile([P, T], U8, name="x_plane", align_bytes=64)
         frac_sb = keep.tile([P, T], F32, name="frac_sb")
+        rest_sb = keep.tile([P, T], F32, name="rest_sb")
 
         identity = keep.tile([P, P], F32, name="identity")
         nc.gpsimd.memset(x_plane[:].bitcast(I32), 0)
         make_identity(nc, identity[:])
 
         w_rows = w1.rearrange("(p j) m -> p j m", j=PACK)
-        w_raw = [keep.tile([P, PACK, W_COLS], F32, name=f"w_raw{c}") for c in range(2)]
+        w_raw = [keep.tile([P, PACK, PACK * (b - a)], F32, name=f"w_raw{c}") for c, (a, b) in enumerate(PIECES[:2])]
+        w_raw.append(laid.tile([P, PACK, PACK * (PIECES[2][1] - PIECES[2][0])], F32, name="w_raw2", offset=0))
 
         def load_w(c):
-            nc.sync.dma_start(out=w_raw[c][:], in_=w_rows[:, :, c * W_COLS : (c + 1) * W_COLS])
+            a, b = PIECES[c]
+            nc.sync.dma_start(out=w_raw[c][:], in_=w_rows[:, :, PACK * a : PACK * b])
 
         nc.sync.dma_start(right_sb[:], right)
         load_w(0)
@@ -67,175 +70,190 @@ def tile_picked_wlerp_none_lo_kernel(
         load_w(1)
         nc.sync.dma_start(out=frac_sb[:], in_=frac)
         nc.sync.dma_start(left_sb[:], left)
+        load_w(2)
 
-        w_early = [keep.tile([P, N], BF16, name=f"w_early{c}", tag=f"w_early{c}", align_bytes=64) for c in range(2)]
-        y = [keep.tile([P, T + SPARE if t == 0 else T], F32, name=f"y{t}") for t in range(PACK)]
+        w_dealt = keep.tile([P, PACK * P * PACK], BF16, name="w_dealt", align_bytes=64)
+        w_turned = w_dealt[:, 0 : TURNED * P * PACK]
+        w_last = w_dealt[:, TURNED * P * PACK :]
+        y = {t: keep.tile([P, T + SPARE if t == 0 else T], F32, name=f"y{t}") for t in range(PACK)}
         nc.gpsimd.memset(y[0][:, T:], 0.0)
 
-        def deal(copy, target, c, t0, i0=0, i1=WORDS):
-            source = w_raw[c][:].rearrange("p j (i t) -> p i j t", t=PACK)
-            dealt = target[:].rearrange("p (t i j) -> p i j t", t=2, j=PACK)
-            copy(dealt[:, i0:i1], source[:, i0:i1, :, t0 : t0 + 2])
+        def deal(copy, c, q0=None, q1=None):
+            a, b = PIECES[c]
+            q0 = a if q0 is None else q0
+            q1 = b if q1 is None else q1
+            source = w_raw[c][:].rearrange("p j (q t) -> p q j t", t=PACK)
+            dealt = w_turned.rearrange("p (q t j) -> p q j t", t=TURNED, j=PACK)
+            copy(dealt[:, q0:q1], source[:, q0 - a : q1 - a, :, 0:TURNED])
 
-        def quantise_early(c):
-            codes = keep.tile([P, P], U32, name=f"w_codes{c}", tag=f"w_codes{c}", align_bytes=64)
-            plane = keep.tile([P, P], U8, name=f"w_plane{c}", tag=f"w_plane{c}", align_bytes=64)
-            nc.vector.quantize_mx(out=codes[:].bitcast(FP8X4), scales=plane[:], in_=w_early[c][:])
-            return codes, plane
+        def deal_last(copy, c):
+            a, b = PIECES[c]
+            source = w_raw[c][:].rearrange("p j (q t) -> p q j t", t=PACK)
+            dealt = w_last.rearrange("p (q j) -> p q j", j=PACK)
+            copy(dealt[:, a:b], source[:, :, :, TURNED])
+
+        def quantise_w(c0, c1):
+            codes = keep.tile([P, (c1 - c0) * P], U32, name=f"w_codes{c0}", align_bytes=64)
+            plane = keep.tile([P, (c1 - c0) * P], U8, name=f"w_plane{c0}", align_bytes=64)
+            nc.vector.quantize_mx(
+                out=codes[:].bitcast(FP8X4), scales=plane[:], in_=w_dealt[:, c0 * P * PACK : c1 * P * PACK]
+            )
+            return [(codes[:, u * P : (u + 1) * P], plane[:, u * P : (u + 1) * P]) for u in range(c1 - c0)]
 
         def project(t, codes, plane, spans):
-            for a, b in spans:
-                acc = psum.tile([P, b - a], F32, name=f"acc{t}_{a}", tag="acc", bufs=4)
+            for a, b, copy, bank in spans:
+                acc = psum.tile([P, b - a], F32, name=f"acc{t}_{a}", tag=f"bank{bank}")
                 nc.tensor.matmul_mx(
                     out=acc[:],
-                    lhsT=codes[:].bitcast(FP8X4),
-                    lhsT_scale=plane[:],
+                    lhsT=codes.bitcast(FP8X4),
+                    lhsT_scale=plane,
                     rhs=x_codes[:, a:b].bitcast(FP8X4),
                     rhs_scale=x_plane[:, a:b],
                     start=True,
                     stop=True,
                 )
-                nc.scalar.copy(out=y[t][:, a:b], in_=acc[:])
+                copy(out=y[t][:, a:b], in_=acc[:])
 
         out_rows = out_0.rearrange("(p t) v -> p t v", t=PACK)
         out_words = out_1[0].rearrange("p c r -> p (c r)").bitcast(I32)
         o_plane = keep.tile([P, T], U8, name="o_plane", align_bytes=64)
-        whole = keep.tile([P, PACK, T], F32, name="whole")
-        mixed = [whole[:, :, h * HALF : (h + 1) * HALF] for h in range(2)]
-        rounded = [keep.tile([P, PACK * HALF], BF16, name=f"rounded{h}", align_bytes=64) for h in range(2)]
+        room = keep.tile([P, PACK * T + 2 * P], F32, name="room", align_bytes=64)
+        whole = room[:, : PACK * T].rearrange("p (t v) -> p t v", t=PACK)
 
-        def fetch(t, a, b, offsets, weight, name):
-            part = keep.tile([P, b - a], F32, name=f"{name}{t}_{a}")
+        def rows(t0, t1, a, b):
+            return whole[:, t0:t1, a:b]
+
+        rounded = {k: keep.tile([P, PACK * P], BF16, name=f"rounded{k}", align_bytes=64)[:] for k in (0, 2, 3)}
+        rounded.setdefault(1, room[:, PACK * T :].bitcast(BF16))
+
+        def fetch(t, a, b, offsets, weight, name, part):
+            if part is None:
+                part = keep.tile([P, b - a], F32, name=f"{name}{t}_{a}")[:]
             listed = y[t][:].indirect(offsets[:, a // LIST_ROWS : b // LIST_ROWS])
-            nc.vector.tensor_tensor(part[:], listed, weight[:, a:b], MULT)
+            nc.vector.tensor_tensor(part, listed, weight[:, a:b], MULT)
             return part
 
-        def fetch_both(t, a, b):
-            return fetch(t, a, b, right_sb, frac_sb, "far"), fetch(t, a, b, left_sb, rest_sb, "near")
+        def far(t, a, b, part=None):
+            return fetch(t, a, b, right_sb, frac_sb, "far", part)
 
-        def turn_and_sum(t, h, terms, first):
-            turned = psum.tile([P, BLOCKS, P], F32, name=f"turned{t}_{h}", tag="turned", bufs=2)
-            for n, term in enumerate(terms):
-                for k in range(BLOCKS):
-                    nc.tensor.matmul(
-                        turned[:, k, :], term[:, first + k * P : first + (k + 1) * P], identity[:],
-                        start=(n == 0 and k == 0), stop=(n == 1 and k == BLOCKS - 1), is_transpose=True,
-                    )
-            return turned
+        def near(t, a, b, part=None):
+            return fetch(t, a, b, left_sb, rest_sb, "near", part)
 
-        def turn_back(t0, t1, h, rows):
-            home = psum.tile([P, t1 - t0, HALF], F32, name=f"home{t0}_{h}", tag="home", bufs=2)
-            for t in range(t0, t1):
-                for k in range(BLOCKS):
-                    nc.tensor.transpose(home[:, t - t0, k * P : (k + 1) * P], rows(t, k), identity[:])
-            nc.scalar.copy(out=mixed[h][:, t0:t1, :], in_=home[:])
+        turned = {}
 
-        def store(h, t0, t1):
-            nc.sync.dma_start(
-                out=out_rows[:, t0:t1, h * HALF : (h + 1) * HALF], in_=mixed[h][:, t0:t1, :]
+        def turn_term(c, k, term, first):
+            if k not in turned:
+                turned.setdefault(k, psum.tile([P, TURNED * P], F32, name=f"turned{k}", tag=f"bank{k}"))
+            nc.tensor.matmul(
+                turned[k][:, c * P : (c + 1) * P], term, identity[:],
+                start=first, stop=not first, is_transpose=True,
             )
 
-        def weave(h, a, b):
-            woven = rounded[h][:, PACK * a : PACK * b].rearrange("p (c i t) -> p c t i", i=PACK, t=PACK)
-            source = mixed[h][:, :, a:b].rearrange("p t (c i) -> p c t i", i=PACK)
+        def turn(c, k, far_cols, near_cols):
+            turn_term(c, k, far_cols, True)
+            turn_term(c, k, near_cols, False)
+
+        def turn_span(c, a, b, far_part, near_part):
+            for k in range(a // P, b // P):
+                cols = slice(k * P - a, (k + 1) * P - a)
+                turn(c, k, far_part[:, cols], near_part[:, cols])
+
+        flat = [keep.tile([P, TURNED * P], F32, name=f"summed{k}")[:] for k in range(T // P - 1)]
+        flat.append(room[:, PACK * T - P :])
+
+        def park(k, q0, q1):
+            summed = flat[k].rearrange("s (t q) -> s t q", t=TURNED)
+            nc.scalar.copy(out=summed[:, :, q0:q1], in_=turned[k][:].rearrange("s (q t) -> s t q", t=TURNED)[:, :, q0:q1])
+
+        def bring_home(k):
+            park(k, EARLY, P)
+            summed = flat[k].rearrange("s (t q) -> s t q", t=TURNED)
+            home = psum.tile([P, TURNED, P], F32, name=f"home{k}", tag=f"bank{4 + k}")
+            for t in range(TURNED):
+                nc.tensor.transpose(home[:, t, :], summed[:, t, :], identity[:])
+            nc.scalar.copy(out=rows(0, TURNED, k * P, (k + 1) * P), in_=home[:])
+            return flat[k]
+
+        def store(t0, t1, a, b):
+            nc.sync.dma_start(out=out_rows[:, t0:t1, a:b], in_=rows(t0, t1, a, b))
+
+        def weave(a, b):
+            woven = rounded[a // P].rearrange("p (c i t) -> p c t i", i=PACK, t=PACK)
+            source = rows(0, PACK, a, b).rearrange("p t (c i) -> p c t i", i=PACK)
             return woven, source
 
-        def quantise_out(h, a, b):
-            codes = keep.tile([P, b - a], U32, name=f"o_codes{h}_{a}", align_bytes=64)
-            cols = slice(h * HALF + a, h * HALF + b)
+        o_codes = [keep.tile([P, HALF], U32, name=f"o_codes{h}", align_bytes=64) for h in range(2)]
+
+        def quantise_out(a, b):
+            h = a // HALF
             nc.vector.quantize_mx(
-                out=codes[:].bitcast(FP8X4), scales=o_plane[:, cols], in_=rounded[h][:, PACK * a : PACK * b]
-            )
-            nc.sync.dma_start(out=out_words[:, cols], in_=codes[:].bitcast(I32))
-
-        early_sum = [keep.tile([P, BLOCKS, 2, P], F32, name=f"early_sum{h}") for h in range(2)]
-
-        def sum_early(c, h, terms, first):
-            turned = turn_and_sum(c, h, terms, first)
-            nc.scalar.copy(
-                out=early_sum[h][:, :, :, WORDS * c : WORDS * (c + 1)],
-                in_=turned[:].rearrange("s k (t i) -> s k t i", t=2),
+                out=o_codes[h][:, a - h * HALF : b - h * HALF].bitcast(FP8X4),
+                scales=o_plane[:, a:b],
+                in_=rounded[a // P],
             )
 
-        deal(nc.vector.tensor_copy, w_early[0], 0, 0, 0, DEAL_CUT)
-        deal(nc.scalar.copy, w_early[0], 0, 0, DEAL_CUT, WORDS)
-        weights0 = quantise_early(0)
-        w_late = [keep.tile([P, N], BF16, name="w_late0", tag="w_early0", align_bytes=64)]
-        late_codes = [keep.tile([P, P], U32, name=f"late_codes{u}", align_bytes=64) for u in range(2)]
-        late_plane = [keep.tile([P, P], U8, name=f"late_plane{u}", align_bytes=64) for u in range(2)]
+        def store_codes(h):
+            nc.sync.dma_start(out=out_words[:, h * HALF : (h + 1) * HALF], in_=o_codes[h][:].bitcast(I32))
 
-        def quantise_late(c):
-            cols = slice(WORDS * c, WORDS * (c + 1))
-            for u in range(2):
-                nc.vector.quantize_mx(
-                    out=late_codes[u][:, cols].bitcast(FP8X4),
-                    scales=late_plane[u][:, cols],
-                    in_=w_late[c][:, u * W_COLS : (u + 1) * W_COLS],
-                )
-
-        deal(nc.vector.tensor_copy, w_late[0], 0, 2)
-        quantise_late(0)
-        deal(nc.vector.tensor_copy, w_early[1], 1, 0)
-        weights1 = quantise_early(1)
-        project(0, *weights0, [(a, a + P) for a in range(0, T, P)])
-        rest_sb = keep.tile([P, T], F32, name="rest_sb", tag="w_plane0", align_bytes=64)
+        deal(nc.vector.tensor_copy, 0, 0, DEAL_CUT)
+        deal(nc.scalar.copy, 0, DEAL_CUT, None)
+        (weights0,) = quantise_w(0, 1)
+        deal_last(nc.vector.tensor_copy, 0)
+        deal(nc.vector.tensor_copy, 1)
+        deal_last(nc.vector.tensor_copy, 1)
+        (weights1,) = quantise_w(1, 2)
+        project(0, *weights0, [(k * P, (k + 1) * P, nc.scalar.copy, 4 + k) for k in range(T // P)])
         nc.scalar.activation(rest_sb[:], frac_sb[:], COPY, bias=1.0, scale=-1.0)
-        project(1, *weights1, [(0, T)])
-        w_late.append(keep.tile([P, N], BF16, name="w_late1", tag="w_codes0", align_bytes=64))
-        deal(nc.scalar.copy, w_late[1], 1, 2)
+        project(1, *weights1, [(0, T, nc.scalar.copy, 4)])
+        deal(nc.scalar.copy, 2)
+        deal_last(nc.scalar.copy, 2)
 
-        terms = fetch_both(0, 0, T)
-        quantise_late(1)
-        for u in range(2):
-            project(2 + u, late_codes[u], late_plane[u], [(0, T)])
-        for h in range(2):
-            sum_early(0, h, terms, h * HALF)
+        def spent(name, n):
+            return laid.tile([P, HALF], F32, name=name, offset=1024 * n)[:]
 
-        for h in range(2):
-            sum_early(1, h, fetch_both(1, h * HALF, (h + 1) * HALF), 0)
-            turn_back(0, 2, h, lambda t, k: early_sum[h][:, k, t, :])
-            if h == 1:
-                store(h, 0, 2)
+        far0, near0 = far(0, 0, T), near(0, 0, T)
+        far1 = far(1, 0, HALF)
+        weights2, weights3 = quantise_w(2, 4)
+        project(2, *weights2, [(0, HALF, nc.scalar.copy, 5), (HALF, T, nc.scalar.copy, 6)])
+        project(3, *weights3, [(0, T, nc.scalar.copy, 7)])
+        turn_span(0, 0, T, far0, near0)
+        turn_span(1, 0, HALF, far1, near(1, 0, HALF, spent("near1a", 0)))
+        turn_span(1, HALF, T, far(1, HALF, T, spent("far1b", 1)), near(1, HALF, T, spent("near1b", 2)))
+        for k in range(T // P):
+            park(k, 0, EARLY)
+        turn_span(2, 0, HALF, far(2, 0, HALF), near(2, 0, HALF))
+        far2 = far(2, HALF, T)
+        for k in (2, 3):
+            turn(2, k, far2[:, k * P - HALF : (k + 1) * P - HALF], near(2, k * P, (k + 1) * P))
+        bring_home(0)
+        bring_home(1)
+        store(0, 2, 0, HALF)
 
-        for h in range(2):
-            turned = turn_and_sum(2, h, fetch_both(2, h * HALF, (h + 1) * HALF), 0)
-            parked = mixed[1][:, 3, :] if h else keep.tile([P, HALF], F32, name="summed0")
-            summed = parked[:].rearrange("s (k p) -> s k p", k=BLOCKS)
-            nc.scalar.copy(out=summed, in_=turned[:])
-            if h == 0:
-                turn_back(2, 3, h, lambda t, k: summed[:, k, :])
-                store(0, 0, 3)
+        def add(a, b, near_part, far_part):
+            nc.vector.tensor_tensor(whole[:, 3, a:b], near_part, far_part, ADD)
 
-        pieces = [(0, P), (P, HALF)]
-
-        def sum_on_vector(h):
-            far = fetch(3, h * HALF, (h + 1) * HALF, right_sb, frac_sb, "far")
-            near = [fetch(3, h * HALF + a, h * HALF + b, left_sb, rest_sb, "near") for a, b in pieces]
-            for (a, b), part in zip(pieces, near):
-                nc.vector.tensor_tensor(mixed[h][:, 3, a:b], part[:], far[:, a:b], ADD)
-            if h == 1:
-                store(h, 3, 4)
-
-        sum_on_vector(0)
-        nc.scalar.copy(*weave(0, 0, P))
-        turn_back(2, 3, 1, lambda t, k: summed[:, k, :])
-        run = slice(2 * T + HALF, 3 * T + HALF)
-        nc.sync.dma_start(
-            out=out_rows.rearrange("p t v -> p (t v)")[:, run], in_=whole[:].rearrange("p t v -> p (t v)")[:, run]
-        )
-        nc.scalar.copy(*weave(0, P, HALF))
-        sum_on_vector(1)
-        nc.vector.tensor_copy(*weave(1, 0, ROUND_CUT))
-        nc.scalar.copy(*weave(1, ROUND_CUT, HALF))
-        quantise_out(0, 0, HALF)
-        codes = keep.tile([P, HALF], U32, name="o_codes_last", align_bytes=64)
-        for a, b in pieces:
-            nc.vector.quantize_mx(
-                out=codes[:, a:b].bitcast(FP8X4),
-                scales=o_plane[:, HALF + a : HALF + b],
-                in_=rounded[1][:, PACK * a : PACK * b],
-            )
-        nc.sync.dma_start(out=out_words[:, HALF:], in_=codes[:].bitcast(I32))
+        terms = [(near(3, k * P, (k + 1) * P), far(3, k * P, (k + 1) * P)) for k in (0, 1)]
+        add(0, P, *terms[0])
+        far3 = far(3, HALF, T)
+        add(P, HALF, *terms[1])
+        store(2, PACK, 0, HALF)
+        nc.scalar.copy(*weave(0, P))
+        bring_home(2)
+        bring_home(3)
+        store(0, TURNED, HALF, T)
+        nc.scalar.copy(*weave(P, HALF))
+        near3 = [near(3, k * P, (k + 1) * P) for k in (2, 3)]
+        add(2 * P, 3 * P, near3[0], far3[:, 0:P])
+        add(3 * P, T, near3[1], far3[:, P:])
+        store(TURNED, PACK, HALF, T)
+        quantise_out(0, P)
+        nc.vector.tensor_copy(*weave(2 * P, 3 * P))
+        nc.vector.tensor_copy(*weave(3 * P, T))
+        quantise_out(2 * P, 3 * P)
+        quantise_out(P, HALF)
+        store_codes(0)
+        quantise_out(3 * P, T)
+        store_codes(1)
         for q in range(4):
             engine = nc.sync if q % 2 == 0 else nc.scalar
             engine.dma_start(

@@ -117,14 +117,11 @@ def tile_picked_wlerp_none_lo_kernel(
         out_rows = out_0.rearrange("(p t) v -> p t v", t=PACK)
         out_words = out_1[0].rearrange("p c r -> p (c r)").bitcast(I32)
         o_plane = keep.tile([P, T], U8, name="o_plane", align_bytes=64)
-        room = keep.tile([P, PACK * T + 2 * P], F32, name="room", align_bytes=64)
-        whole = room[:, : PACK * T].rearrange("p (t v) -> p t v", t=PACK)
+        whole = keep.tile([P, PACK, T], F32, name="whole")
 
         def rows(t0, t1, a, b):
             return whole[:, t0:t1, a:b]
 
-        rounded = {k: keep.tile([P, PACK * P], BF16, name=f"rounded{k}", align_bytes=64)[:] for k in (0, 2, 3)}
-        rounded.setdefault(1, room[:, PACK * T :].bitcast(BF16))
 
         def fetch(t, a, b, offsets, weight, name, part):
             if part is None:
@@ -159,7 +156,11 @@ def tile_picked_wlerp_none_lo_kernel(
                 turn(c, k, far_part[:, cols], near_part[:, cols])
 
         flat = [keep.tile([P, TURNED * P], F32, name=f"summed{k}")[:] for k in range(T // P - 1)]
-        flat.append(room[:, PACK * T - P :])
+        flat.append(laid.tile([P, TURNED * P], F32, name="summed3", offset=4096)[:])
+
+        rounded = {k: keep.tile([P, PACK * P], BF16, name=f"rounded{k}", align_bytes=64)[:] for k in (2, 3)}
+        for k in (0, 1):
+            rounded.setdefault(k, laid.tile([P, PACK * P], BF16, name=f"rounded{k}", align_bytes=64, offset=4096 + 1024 * k)[:])
 
         def park(k, q0, q1):
             summed = flat[k].rearrange("s (t q) -> s t q", t=TURNED)
@@ -178,22 +179,18 @@ def tile_picked_wlerp_none_lo_kernel(
             nc.sync.dma_start(out=out_rows[:, t0:t1, a:b], in_=rows(t0, t1, a, b))
 
         def weave(a, b):
-            woven = rounded[a // P].rearrange("p (c i t) -> p c t i", i=PACK, t=PACK)
+            woven = rounded[a // P][:, PACK * (a % P) : PACK * ((b - 1) % P + 1)].rearrange("p (c i t) -> p c t i", i=PACK, t=PACK)
             source = rows(0, PACK, a, b).rearrange("p t (c i) -> p c t i", i=PACK)
             return woven, source
 
-        o_codes = [keep.tile([P, HALF], U32, name=f"o_codes{h}", align_bytes=64) for h in range(2)]
+        o_codes = keep.tile([P, T], U32, name="o_codes", align_bytes=64)
 
         def quantise_out(a, b):
-            h = a // HALF
             nc.vector.quantize_mx(
-                out=o_codes[h][:, a - h * HALF : b - h * HALF].bitcast(FP8X4),
+                out=o_codes[:, a:b].bitcast(FP8X4),
                 scales=o_plane[:, a:b],
                 in_=rounded[a // P],
             )
-
-        def store_codes(h):
-            nc.sync.dma_start(out=out_words[:, h * HALF : (h + 1) * HALF], in_=o_codes[h][:].bitcast(I32))
 
         deal(nc.vector.tensor_copy, 0, 0, DEAL_CUT)
         deal(nc.scalar.copy, 0, DEAL_CUT, None)
@@ -227,7 +224,10 @@ def tile_picked_wlerp_none_lo_kernel(
             turn(2, k, far2[:, k * P - HALF : (k + 1) * P - HALF], near(2, k * P, (k + 1) * P))
         bring_home(0)
         bring_home(1)
-        store(0, 2, 0, HALF)
+        store(0, TURNED, 0, HALF)
+        bring_home(2)
+        bring_home(3)
+        store(0, 2, HALF, T)
 
         def add(a, b, near_part, far_part):
             nc.vector.tensor_tensor(whole[:, 3, a:b], near_part, far_part, ADD)
@@ -236,24 +236,23 @@ def tile_picked_wlerp_none_lo_kernel(
         add(0, P, *terms[0])
         far3 = far(3, HALF, T)
         add(P, HALF, *terms[1])
-        store(2, PACK, 0, HALF)
         nc.scalar.copy(*weave(0, P))
-        bring_home(2)
-        bring_home(3)
-        store(0, TURNED, HALF, T)
         nc.scalar.copy(*weave(P, HALF))
         near3 = [near(3, k * P, (k + 1) * P) for k in (2, 3)]
         add(2 * P, 3 * P, near3[0], far3[:, 0:P])
         add(3 * P, T, near3[1], far3[:, P:])
-        store(TURNED, PACK, HALF, T)
-        quantise_out(0, P)
+        run = slice(2 * T + HALF, PACK * T)
+        nc.sync.dma_start(
+            out=out_rows.rearrange("p t v -> p (t v)")[:, run], in_=whole[:].rearrange("p t v -> p (t v)")[:, run]
+        )
         nc.vector.tensor_copy(*weave(2 * P, 3 * P))
-        nc.vector.tensor_copy(*weave(3 * P, T))
+        nc.vector.tensor_copy(*weave(3 * P, T - 64))
+        nc.scalar.copy(*weave(T - 64, T))
         quantise_out(2 * P, 3 * P)
-        quantise_out(P, HALF)
-        store_codes(0)
+        quantise_out(0, P)
         quantise_out(3 * P, T)
-        store_codes(1)
+        quantise_out(P, HALF)
+        nc.sync.dma_start(out=out_words, in_=o_codes[:].bitcast(I32))
         for q in range(4):
             engine = nc.sync if q % 2 == 0 else nc.scalar
             engine.dma_start(

@@ -175,8 +175,11 @@ def tile_picked_wlerp_none_lo_kernel(
             nc.scalar.copy(out=rows(0, TURNED, k * P, (k + 1) * P), in_=home[:])
             return flat[k]
 
-        def store(t0, t1, a, b):
-            nc.sync.dma_start(out=out_rows[:, t0:t1, a:b], in_=rows(t0, t1, a, b))
+        def store_run(t):
+            run = slice(t * T + HALF, (t + 2) * T)
+            nc.sync.dma_start(
+                out=out_rows.rearrange("p t v -> p (t v)")[:, run], in_=whole[:].rearrange("p t v -> p (t v)")[:, run]
+            )
 
         def weave(a, b):
             woven = rounded[a // P][:, PACK * (a % P) : PACK * ((b - 1) % P + 1)].rearrange("p (c i t) -> p c t i", i=PACK, t=PACK)
@@ -224,10 +227,10 @@ def tile_picked_wlerp_none_lo_kernel(
             turn(2, k, far2[:, k * P - HALF : (k + 1) * P - HALF], near(2, k * P, (k + 1) * P))
         bring_home(0)
         bring_home(1)
-        store(0, TURNED, 0, HALF)
+        nc.sync.dma_start(out=out_rows[:, 0:PACK:2, 0:HALF], in_=whole[:, 0:PACK:2, 0:HALF])
         bring_home(2)
         bring_home(3)
-        store(0, 2, HALF, T)
+        store_run(0)
 
         def add(a, b, near_part, far_part):
             nc.vector.tensor_tensor(whole[:, 3, a:b], near_part, far_part, ADD)
@@ -241,10 +244,7 @@ def tile_picked_wlerp_none_lo_kernel(
         near3 = [near(3, k * P, (k + 1) * P) for k in (2, 3)]
         add(2 * P, 3 * P, near3[0], far3[:, 0:P])
         add(3 * P, T, near3[1], far3[:, P:])
-        run = slice(2 * T + HALF, PACK * T)
-        nc.sync.dma_start(
-            out=out_rows.rearrange("p t v -> p (t v)")[:, run], in_=whole[:].rearrange("p t v -> p (t v)")[:, run]
-        )
+        store_run(2)
         nc.vector.tensor_copy(*weave(2 * P, 3 * P))
         nc.vector.tensor_copy(*weave(3 * P, T - 64))
         nc.scalar.copy(*weave(T - 64, T))

@@ -158,9 +158,13 @@ def tile_picked_wlerp_none_lo_kernel(
         flat = [keep.tile([P, TURNED * P], F32, name=f"summed{k}")[:] for k in range(T // P - 1)]
         flat.append(laid.tile([P, TURNED * P], F32, name="summed3", offset=4096)[:])
 
-        rounded = {k: keep.tile([P, PACK * P], BF16, name=f"rounded{k}", align_bytes=64)[:] for k in (2, 3)}
-        for k in (0, 1):
-            rounded.setdefault(k, laid.tile([P, PACK * P], BF16, name=f"rounded{k}", align_bytes=64, offset=4096 + 1024 * k)[:])
+        rounded = [
+            laid.tile([P, PACK * HALF], BF16, name="rounded0", align_bytes=64, offset=4096),
+            keep.tile([P, PACK * HALF], BF16, name="rounded1", align_bytes=64),
+        ]
+
+        def rounded_span(a, b):
+            return rounded[a // HALF][:, PACK * (a % HALF) : PACK * ((b - 1) % HALF + 1)]
 
         def park(k, q0, q1):
             summed = flat[k].rearrange("s (t q) -> s t q", t=TURNED)
@@ -182,7 +186,7 @@ def tile_picked_wlerp_none_lo_kernel(
             )
 
         def weave(a, b):
-            woven = rounded[a // P][:, PACK * (a % P) : PACK * ((b - 1) % P + 1)].rearrange("p (c i t) -> p c t i", i=PACK, t=PACK)
+            woven = rounded_span(a, b).rearrange("p (c i t) -> p c t i", i=PACK, t=PACK)
             source = rows(0, PACK, a, b).rearrange("p t (c i) -> p c t i", i=PACK)
             return woven, source
 
@@ -192,7 +196,7 @@ def tile_picked_wlerp_none_lo_kernel(
             nc.vector.quantize_mx(
                 out=o_codes[:, a:b].bitcast(FP8X4),
                 scales=o_plane[:, a:b],
-                in_=rounded[a // P],
+                in_=rounded_span(a, b),
             )
 
         deal(nc.vector.tensor_copy, 0, 0, DEAL_CUT)
@@ -235,24 +239,20 @@ def tile_picked_wlerp_none_lo_kernel(
         def add(a, b, near_part, far_part):
             nc.vector.tensor_tensor(whole[:, 3, a:b], near_part, far_part, ADD)
 
-        terms = [(near(3, k * P, (k + 1) * P), far(3, k * P, (k + 1) * P)) for k in (0, 1)]
-        add(0, P, *terms[0])
+        terms = near(3, 0, HALF), far(3, 0, HALF)
         far3 = far(3, HALF, T)
-        add(P, HALF, *terms[1])
-        nc.scalar.copy(*weave(0, P))
-        nc.scalar.copy(*weave(P, HALF))
+        add(0, HALF, *terms)
+        nc.scalar.copy(*weave(0, HALF))
         near3 = [near(3, k * P, (k + 1) * P) for k in (2, 3)]
         add(2 * P, 3 * P, near3[0], far3[:, 0:P])
         add(3 * P, T, near3[1], far3[:, P:])
         store_run(2)
-        nc.vector.tensor_copy(*weave(2 * P, 3 * P))
+        nc.vector.tensor_copy(*weave(HALF, 3 * P))
         nc.vector.tensor_copy(*weave(3 * P, T - 64))
         nc.scalar.copy(*weave(T - 64, T))
-        quantise_out(2 * P, 3 * P)
-        quantise_out(0, P)
-        quantise_out(3 * P, T)
-        quantise_out(P, HALF)
-        nc.sync.dma_start(out=out_words, in_=o_codes[:].bitcast(I32))
+        for a in (0, HALF):
+            quantise_out(a, a + HALF)
+            nc.sync.dma_start(out=out_words[:, a : a + HALF], in_=o_codes[:, a : a + HALF].bitcast(I32))
         for q in range(4):
             engine = nc.sync if q % 2 == 0 else nc.scalar
             engine.dma_start(

@@ -1,7 +1,6 @@
 from contextlib import ExitStack
 
 import concourse.mybir as mybir
-from concourse.masks import make_identity
 
 K, T, N = 512, 512, 512
 FLOPS = 2 * K * T * N
@@ -20,12 +19,8 @@ COPY = mybir.ActivationFunctionType.Copy
 P = 128
 PACK = 4
 LIST_ROWS = 16
-SPARE = 16
 HALF = T // 2
-TURNED = 3
-PIECES = [(0, 44), (44, 88), (88, 128)]
-DEAL_CUT = 28
-EARLY = 2 * P // TURNED
+PIECES = [(0, 64), (64, 128)]
 
 
 def tile_picked_wlerp_none_lo_kernel(
@@ -34,7 +29,6 @@ def tile_picked_wlerp_none_lo_kernel(
     nc = tc.nc
     with ExitStack() as ctx:
         keep = ctx.enter_context(tc.tile_pool(name="keep", bufs=1))
-        laid = ctx.enter_context(tc.tile_pool(name="laid", bufs=1))
         psum = ctx.enter_context(tc.psum_pool(name="psum", bufs=1))
 
         left_sb = keep.tile([P, T // LIST_ROWS], U16, name="left_sb")
@@ -43,216 +37,170 @@ def tile_picked_wlerp_none_lo_kernel(
         x_plane = keep.tile([P, T], U8, name="x_plane", align_bytes=64)
         frac_sb = keep.tile([P, T], F32, name="frac_sb")
         rest_sb = keep.tile([P, T], F32, name="rest_sb")
-
-        identity = keep.tile([P, P], F32, name="identity")
-        nc.gpsimd.memset(x_plane[:].bitcast(I32), 0)
-        make_identity(nc, identity[:])
+        nc.vector.memset(x_plane[:].bitcast(I32), 0)
 
         w_rows = w1.rearrange("(p j) m -> p j m", j=PACK)
-        w_raw = [keep.tile([P, PACK, PACK * (b - a)], F32, name=f"w_raw{c}") for c, (a, b) in enumerate(PIECES[:2])]
-        w_raw.append(laid.tile([P, PACK, PACK * (PIECES[2][1] - PIECES[2][0])], F32, name="w_raw2", offset=0))
+        w_raw = [keep.tile([P, PACK, PACK * (b - a)], F32, name=f"w_raw{c}") for c, (a, b) in enumerate(PIECES)]
 
         def load_w(c):
             a, b = PIECES[c]
             nc.sync.dma_start(out=w_raw[c][:], in_=w_rows[:, :, PACK * a : PACK * b])
 
+        def load_scales(q, engine):
+            engine.dma_start(
+                out=x_plane[32 * q : 32 * q + 4, :].bitcast(I32),
+                in_=x_scales[0, 4 * q : 4 * q + 4, :].bitcast(I32),
+            )
+
+        nc.sync.dma_start(left_sb[:], left)
         nc.sync.dma_start(right_sb[:], right)
         load_w(0)
+        load_w(1)
         nc.sync.dma_start(
             out=x_codes[:].bitcast(I32),
             in_=x_words[0].rearrange("p c r -> p (c r)").bitcast(I32),
         )
         for q in range(4):
-            (nc.scalar if q < 2 else nc.sync).dma_start(
-                out=x_plane[32 * q : 32 * q + 4, :].bitcast(I32),
-                in_=x_scales[0, 4 * q : 4 * q + 4, :].bitcast(I32),
-            )
-        load_w(1)
+            load_scales(q, nc.sync)
         nc.sync.dma_start(out=frac_sb[:], in_=frac)
-        nc.sync.dma_start(left_sb[:], left)
-        load_w(2)
 
-        w_dealt = keep.tile([P, PACK * P * PACK], BF16, name="w_dealt", align_bytes=64)
-        w_turned = w_dealt[:, 0 : TURNED * P * PACK]
-        w_last = w_dealt[:, TURNED * P * PACK :]
-        y = {t: keep.tile([P, T + SPARE if t == 0 else T], F32, name=f"y{t}") for t in range(PACK)}
-        nc.gpsimd.memset(y[0][:, T:], 0.0)
+        w_dealt = [keep.tile([P, PACK * 64 * PACK], BF16, name=f"w_dealt{u}", align_bytes=64) for u in range(2)]
+        w_codes = [keep.tile([P, P], U32, name=f"w_codes{t}", align_bytes=64) for t in range(PACK)]
+        w_plane = [keep.tile([P, P], U8, name=f"w_plane{t}", align_bytes=64) for t in range(PACK)]
+        y = [keep.tile([P, T], F32, name=f"y{t}") for t in range(PACK)]
 
-        def deal(copy, c, q0=None, q1=None):
-            a, b = PIECES[c]
-            q0 = a if q0 is None else q0
-            q1 = b if q1 is None else q1
+        def deal(copy, c, q0, q1):
+            a = PIECES[c][0]
+            u = a // 64
             source = w_raw[c][:].rearrange("p j (q t) -> p q j t", t=PACK)
-            dealt = w_turned.rearrange("p (q t j) -> p q j t", t=TURNED, j=PACK)
-            copy(dealt[:, q0:q1], source[:, q0 - a : q1 - a, :, 0:TURNED])
+            dealt = w_dealt[u][:].rearrange("p (t q j) -> p q j t", t=PACK, j=PACK)
+            copy(dealt[:, q0 - 64 * u : q1 - 64 * u], source[:, q0 - a : q1 - a])
 
-        def deal_last(copy, c):
-            a, b = PIECES[c]
-            source = w_raw[c][:].rearrange("p j (q t) -> p q j t", t=PACK)
-            dealt = w_last.rearrange("p (q j) -> p q j", j=PACK)
-            copy(dealt[:, a:b], source[:, :, :, TURNED])
-
-        def quantise_w(c0, c1):
-            codes = keep.tile([P, (c1 - c0) * P], U32, name=f"w_codes{c0}", align_bytes=64)
-            plane = keep.tile([P, (c1 - c0) * P], U8, name=f"w_plane{c0}", align_bytes=64)
+        def quantise_w(u, t):
             nc.vector.quantize_mx(
-                out=codes[:].bitcast(FP8X4), scales=plane[:], in_=w_dealt[:, c0 * P * PACK : c1 * P * PACK]
+                out=w_codes[t][:, 64 * u : 64 * u + 64].bitcast(FP8X4),
+                scales=w_plane[t][:, 64 * u : 64 * u + 64],
+                in_=w_dealt[u][:, t * 256 : (t + 1) * 256],
             )
-            return [(codes[:, u * P : (u + 1) * P], plane[:, u * P : (u + 1) * P]) for u in range(c1 - c0)]
 
-        def project(t, codes, plane, spans):
-            for a, b, copy, bank in spans:
-                acc = psum.tile([P, b - a], F32, name=f"acc{t}_{a}", tag=f"bank{bank}")
-                nc.tensor.matmul_mx(
-                    out=acc[:],
-                    lhsT=codes.bitcast(FP8X4),
-                    lhsT_scale=plane,
-                    rhs=x_codes[:, a:b].bitcast(FP8X4),
-                    rhs_scale=x_plane[:, a:b],
-                    start=True,
-                    stop=True,
-                )
-                copy(out=y[t][:, a:b], in_=acc[:])
+        def product(t, a, b, bank):
+            acc = psum.tile([P, b - a], F32, name=f"acc{t}_{a}", tag=f"bank{bank}")
+            nc.tensor.matmul_mx(
+                out=acc[:],
+                lhsT=w_codes[t][:].bitcast(FP8X4),
+                lhsT_scale=w_plane[t][:],
+                rhs=x_codes[:, a:b].bitcast(FP8X4),
+                rhs_scale=x_plane[:, a:b],
+                start=True,
+                stop=True,
+            )
+            return acc
 
         out_rows = out_0.rearrange("(p t) v -> p t v", t=PACK)
         out_words = out_1[0].rearrange("p c r -> p (c r)").bitcast(I32)
         o_plane = keep.tile([P, T], U8, name="o_plane", align_bytes=64)
+        o_codes = keep.tile([P, T], U32, name="o_codes", align_bytes=64)
         whole = keep.tile([P, PACK, T], F32, name="whole")
+        lefts = keep.tile([P, PACK, T], F32, name="lefts")
+        nears = keep.tile([P, PACK, T], F32, name="nears")
+        rights = keep.tile([P, PACK, T], F32, name="rights")
+        fars = keep.tile([P, PACK, T], F32, name="fars")
+        rounded = [keep.tile([P, PACK * HALF], BF16, name=f"rounded{h}", align_bytes=64) for h in range(2)]
 
-        def rows(t0, t1, a, b):
-            return whole[:, t0:t1, a:b]
+        def listed(t, offsets, a, b):
+            return y[t][:].indirect(offsets[:, a // LIST_ROWS : b // LIST_ROWS])
 
+        def fetch_left(t, a, b):
+            nc.scalar.activation(lefts[:, t, a:b], listed(t, left_sb, a, b), COPY)
 
-        def fetch(t, a, b, offsets, weight, name, part):
-            if part is None:
-                part = keep.tile([P, b - a], F32, name=f"{name}{t}_{a}")[:]
-            listed = y[t][:].indirect(offsets[:, a // LIST_ROWS : b // LIST_ROWS])
-            nc.vector.tensor_tensor(part, listed, weight[:, a:b], MULT)
-            return part
+        def fetch_right(t, a, b):
+            nc.scalar.activation(rights[:, t, a:b], listed(t, right_sb, a, b), COPY)
 
-        def far(t, a, b, part=None):
-            return fetch(t, a, b, right_sb, frac_sb, "far", part)
+        def far(t, a, b):
+            nc.vector.tensor_tensor(fars[:, t, a:b], listed(t, right_sb, a, b), frac_sb[:, a:b], MULT)
 
-        def near(t, a, b, part=None):
-            return fetch(t, a, b, left_sb, rest_sb, "near", part)
+        def weigh(terms, fetched, weight, t0, t1, a, b):
+            spread = weight[:, a:b].unsqueeze(1).to_broadcast([P, t1 - t0, b - a])
+            nc.vector.tensor_tensor(terms[:, t0:t1, a:b], fetched[:, t0:t1, a:b], spread, MULT)
 
-        turned = {}
+        def near(t0, t1, a, b):
+            weigh(nears, lefts, rest_sb, t0, t1, a, b)
 
-        def turn_term(c, k, term, first):
-            if k not in turned:
-                turned.setdefault(k, psum.tile([P, TURNED * P], F32, name=f"turned{k}", tag=f"bank{k}"))
-            nc.tensor.matmul(
-                turned[k][:, c * P : (c + 1) * P], term, identity[:],
-                start=first, stop=not first, is_transpose=True,
-            )
-
-        def turn(c, k, far_cols, near_cols):
-            turn_term(c, k, far_cols, True)
-            turn_term(c, k, near_cols, False)
-
-        def turn_span(c, a, b, far_part, near_part):
-            for k in range(a // P, b // P):
-                cols = slice(k * P - a, (k + 1) * P - a)
-                turn(c, k, far_part[:, cols], near_part[:, cols])
-
-        flat = [keep.tile([P, TURNED * P], F32, name=f"summed{k}")[:] for k in range(T // P - 1)]
-        flat.append(laid.tile([P, TURNED * P], F32, name="summed3", offset=4096)[:])
-
-        rounded = [
-            laid.tile([P, PACK * HALF], BF16, name="rounded0", align_bytes=64, offset=4096),
-            keep.tile([P, PACK * HALF], BF16, name="rounded1", align_bytes=64),
-        ]
-
-        def rounded_span(a, b):
-            return rounded[a // HALF][:, PACK * (a % HALF) : PACK * ((b - 1) % HALF + 1)]
-
-        def park(k, q0, q1):
-            summed = flat[k].rearrange("s (t q) -> s t q", t=TURNED)
-            nc.scalar.copy(out=summed[:, :, q0:q1], in_=turned[k][:].rearrange("s (q t) -> s t q", t=TURNED)[:, :, q0:q1])
-
-        def bring_home(k):
-            park(k, EARLY, P)
-            summed = flat[k].rearrange("s (t q) -> s t q", t=TURNED)
-            home = psum.tile([P, TURNED, P], F32, name=f"home{k}", tag=f"bank{4 + k}")
-            for t in range(TURNED):
-                nc.tensor.transpose(home[:, t, :], summed[:, t, :], identity[:])
-            nc.scalar.copy(out=rows(0, TURNED, k * P, (k + 1) * P), in_=home[:])
-            return flat[k]
-
-        def store_run(t):
-            run = slice(t * T + HALF, (t + 2) * T)
-            nc.sync.dma_start(
-                out=out_rows.rearrange("p t v -> p (t v)")[:, run], in_=whole[:].rearrange("p t v -> p (t v)")[:, run]
-            )
+        def add(t0, t1, a, b):
+            nc.vector.tensor_tensor(whole[:, t0:t1, a:b], nears[:, t0:t1, a:b], fars[:, t0:t1, a:b], ADD)
 
         def weave(a, b):
-            woven = rounded_span(a, b).rearrange("p (c i t) -> p c t i", i=PACK, t=PACK)
-            source = rows(0, PACK, a, b).rearrange("p t (c i) -> p c t i", i=PACK)
-            return woven, source
+            h = a // HALF
+            woven = rounded[h][:, PACK * (a - h * HALF) : PACK * (b - h * HALF)]
+            source = whole[:, :, a:b].rearrange("p t (c i) -> p c t i", i=PACK)
+            return woven.rearrange("p (c i t) -> p c t i", i=PACK, t=PACK), source
 
-        o_codes = keep.tile([P, T], U32, name="o_codes", align_bytes=64)
+        def store(t0, t1, a, b):
+            nc.sync.dma_start(out=out_rows[:, t0:t1, a:b], in_=whole[:, t0:t1, a:b])
 
-        def quantise_out(a, b):
-            nc.vector.quantize_mx(
-                out=o_codes[:, a:b].bitcast(FP8X4),
-                scales=o_plane[:, a:b],
-                in_=rounded_span(a, b),
-            )
+        def quantise_out(h):
+            cols = slice(h * HALF, (h + 1) * HALF)
+            nc.vector.quantize_mx(out=o_codes[:, cols].bitcast(FP8X4), scales=o_plane[:, cols], in_=rounded[h][:])
+            nc.sync.dma_start(out=out_words[:, cols], in_=o_codes[:, cols].bitcast(I32))
 
-        deal(nc.vector.tensor_copy, 0, 0, DEAL_CUT)
-        deal(nc.scalar.copy, 0, DEAL_CUT, None)
-        (weights0,) = quantise_w(0, 1)
-        deal_last(nc.vector.tensor_copy, 0)
-        deal(nc.vector.tensor_copy, 1)
-        deal_last(nc.vector.tensor_copy, 1)
-        (weights1,) = quantise_w(1, 2)
-        project(0, *weights0, [(k * P, (k + 1) * P, nc.scalar.copy, 4 + k) for k in range(T // P)])
-        nc.scalar.activation(rest_sb[:], frac_sb[:], COPY, bias=1.0, scale=-1.0)
-        project(1, *weights1, [(0, T, nc.scalar.copy, 4)])
-        deal(nc.scalar.copy, 2)
-        deal_last(nc.scalar.copy, 2)
+        def project(t):
+            nc.scalar.copy(out=y[t][:], in_=product(t, 0, T, 1 + t)[:])
 
-        def spent(name, n):
-            return laid.tile([P, HALF], F32, name=name, offset=1024 * n)[:]
+        deal(nc.vector.tensor_copy, 0, 0, 40)
+        deal(nc.scalar.copy, 0, 40, 64)
+        for t in range(PACK):
+            quantise_w(0, t)
+        deal(nc.vector.tensor_copy, 1, 64, 102)
+        deal(nc.scalar.copy, 1, 102, 128)
+        for t in range(PACK):
+            quantise_w(1, t)
+        nc.vector.tensor_scalar(rest_sb[:], frac_sb[:], -1.0, 1.0, MULT, ADD)
 
-        far0, near0 = far(0, 0, T), near(0, 0, T)
-        far1 = far(1, 0, HALF)
-        weights2, weights3 = quantise_w(2, 4)
-        project(2, *weights2, [(0, HALF, nc.scalar.copy, 5), (HALF, T, nc.scalar.copy, 6)])
-        project(3, *weights3, [(0, T, nc.scalar.copy, 7)])
-        turn_span(0, 0, T, far0, near0)
-        turn_span(1, 0, HALF, far1, near(1, 0, HALF, spent("near1a", 0)))
-        turn_span(1, HALF, T, far(1, HALF, T, spent("far1b", 1)), near(1, HALF, T, spent("near1b", 2)))
-        for k in range(T // P):
-            park(k, 0, EARLY)
-        turn_span(2, 0, HALF, far(2, 0, HALF), near(2, 0, HALF))
-        far2 = far(2, HALF, T)
-        for k in (2, 3):
-            turn(2, k, far2[:, k * P - HALF : (k + 1) * P - HALF], near(2, k * P, (k + 1) * P))
-        bring_home(0)
-        bring_home(1)
-        nc.sync.dma_start(out=out_rows[:, 0:PACK:2, 0:HALF], in_=whole[:, 0:PACK:2, 0:HALF])
-        bring_home(2)
-        bring_home(3)
-        store_run(0)
-
-        def add(a, b, near_part, far_part):
-            nc.vector.tensor_tensor(whole[:, 3, a:b], near_part, far_part, ADD)
-
-        terms = near(3, 0, HALF), far(3, 0, HALF)
-        far3 = far(3, HALF, T)
-        add(0, HALF, *terms)
+        acc = product(0, 0, HALF, 0)
+        nc.scalar.copy(out=y[0][:, 0:HALF], in_=acc[:])
+        acc = product(0, HALF, T, 1)
+        nc.vector.tensor_copy(out=y[0][:, HALF:T], in_=acc[:])
+        fetch_left(0, 0, HALF)
+        fetch_left(0, HALF, T)
+        far(0, 0, HALF)
+        far(0, HALF, T)
+        project(1)
+        project(2)
+        near(0, 1, 0, T)
+        far(1, 0, HALF)
+        add(0, 1, 0, T)
+        store(0, 1, 0, T)
+        fetch_left(1, 0, HALF)
+        fetch_left(1, HALF, T)
+        far(2, 0, HALF)
+        near(1, 2, 0, T)
+        project(3)
+        fetch_right(1, HALF, T)
+        far(3, 0, HALF)
+        weigh(fars, rights, frac_sb, 1, 2, HALF, T)
+        fetch_left(2, 0, HALF)
+        fetch_left(3, 0, HALF)
+        far(3, HALF, T)
+        add(1, 2, 0, T)
+        store(1, 2, 0, T)
+        near(2, 4, 0, HALF)
+        fetch_right(2, HALF, T)
+        fetch_left(2, HALF, T)
+        fetch_left(3, HALF, T)
+        weigh(fars, rights, frac_sb, 2, 3, HALF, T)
+        add(2, 4, 0, HALF)
+        store(2, 4, 0, HALF)
         nc.scalar.copy(*weave(0, HALF))
-        near3 = [near(3, k * P, (k + 1) * P) for k in (2, 3)]
-        add(2 * P, 3 * P, near3[0], far3[:, 0:P])
-        add(3 * P, T, near3[1], far3[:, P:])
-        store_run(2)
-        nc.vector.tensor_copy(*weave(HALF, 3 * P))
-        nc.vector.tensor_copy(*weave(3 * P, T - 64))
-        nc.scalar.copy(*weave(T - 64, T))
-        for a in (0, HALF):
-            quantise_out(a, a + HALF)
-            nc.sync.dma_start(out=out_words[:, a : a + HALF], in_=o_codes[:, a : a + HALF].bitcast(I32))
+        near(2, 4, HALF, 3 * P)
+        near(2, 4, 3 * P, T)
+        add(2, 4, HALF, 3 * P)
+        add(2, 4, 3 * P, T)
+        store(2, 4, HALF, T)
+        nc.scalar.copy(*weave(HALF, HALF + 96))
+        quantise_out(0)
+        nc.vector.tensor_copy(*weave(HALF + 96, 3 * P))
+        nc.vector.tensor_copy(*weave(3 * P, T))
+        quantise_out(1)
         for q in range(4):
             engine = nc.sync if q % 2 == 0 else nc.scalar
             engine.dma_start(

@@ -1,6 +1,7 @@
 from contextlib import ExitStack
 
 import concourse.mybir as mybir
+from concourse.masks import make_identity
 
 K, T, N = 512, 512, 512
 FLOPS = 2 * K * T * N
@@ -14,12 +15,14 @@ U8 = mybir.dt.uint8
 FP8X4 = mybir.dt.float8_e4m3fn_x4
 MULT = mybir.AluOpType.mult
 ADD = mybir.AluOpType.add
+SUB = mybir.AluOpType.subtract
 COPY = mybir.ActivationFunctionType.Copy
 
 P = 128
 PACK = 4
 LIST_ROWS = 16
 HALF = T // 2
+SPARE = 16
 PIECES = [(0, 64), (64, 128)]
 
 
@@ -29,6 +32,7 @@ def tile_picked_wlerp_none_lo_kernel(
     nc = tc.nc
     with ExitStack() as ctx:
         keep = ctx.enter_context(tc.tile_pool(name="keep", bufs=1))
+        laid = ctx.enter_context(tc.tile_pool(name="laid", bufs=1))
         psum = ctx.enter_context(tc.psum_pool(name="psum", bufs=1))
 
         left_sb = keep.tile([P, T // LIST_ROWS], U16, name="left_sb")
@@ -37,7 +41,9 @@ def tile_picked_wlerp_none_lo_kernel(
         x_plane = keep.tile([P, T], U8, name="x_plane", align_bytes=64)
         frac_sb = keep.tile([P, T], F32, name="frac_sb")
         rest_sb = keep.tile([P, T], F32, name="rest_sb")
+        identity = keep.tile([P, P], F32, name="identity")
         nc.vector.memset(x_plane[:].bitcast(I32), 0)
+        make_identity(nc, identity[:])
 
         w_rows = w1.rearrange("(p j) m -> p j m", j=PACK)
         w_raw = [keep.tile([P, PACK, PACK * (b - a)], F32, name=f"w_raw{c}") for c, (a, b) in enumerate(PIECES)]
@@ -53,7 +59,6 @@ def tile_picked_wlerp_none_lo_kernel(
             )
 
         nc.sync.dma_start(left_sb[:], left)
-        nc.sync.dma_start(right_sb[:], right)
         load_w(0)
         load_w(1)
         nc.sync.dma_start(
@@ -63,11 +68,13 @@ def tile_picked_wlerp_none_lo_kernel(
         for q in range(4):
             load_scales(q, nc.sync)
         nc.sync.dma_start(out=frac_sb[:], in_=frac)
+        nc.sync.dma_start(right_sb[:], right)
 
         w_dealt = [keep.tile([P, PACK * 64 * PACK], BF16, name=f"w_dealt{u}", align_bytes=64) for u in range(2)]
         w_codes = [keep.tile([P, P], U32, name=f"w_codes{t}", align_bytes=64) for t in range(PACK)]
         w_plane = [keep.tile([P, P], U8, name=f"w_plane{t}", align_bytes=64) for t in range(PACK)]
-        y = [keep.tile([P, T], F32, name=f"y{t}") for t in range(PACK)]
+        y = [keep.tile([P, T + SPARE if t == 1 else T], F32, name=f"y{t}") for t in range(PACK)]
+        nc.gpsimd.memset(y[1][:, T:], 0.0)
 
         def deal(copy, c, q0, q1):
             a = PIECES[c][0]
@@ -105,7 +112,10 @@ def tile_picked_wlerp_none_lo_kernel(
         nears = keep.tile([P, PACK, T], F32, name="nears")
         rights = keep.tile([P, PACK, T], F32, name="rights")
         fars = keep.tile([P, PACK, T], F32, name="fars")
-        rounded = [keep.tile([P, PACK * HALF], BF16, name=f"rounded{h}", align_bytes=64) for h in range(2)]
+        rounded = [
+            laid.tile([P, PACK * HALF], BF16, name="rounded0", align_bytes=64, offset=1536),
+            keep.tile([P, PACK * HALF], BF16, name="rounded1", align_bytes=64),
+        ]
 
         def listed(t, offsets, a, b):
             return y[t][:].indirect(offsets[:, a // LIST_ROWS : b // LIST_ROWS])
@@ -118,6 +128,33 @@ def tile_picked_wlerp_none_lo_kernel(
 
         def far(t, a, b):
             nc.vector.tensor_tensor(fars[:, t, a:b], listed(t, right_sb, a, b), frac_sb[:, a:b], MULT)
+
+        def near_fused(t, a, b):
+            nc.vector.tensor_tensor(nears[:, t, a:b], listed(t, left_sb, a, b), rest_sb[:, a:b], MULT)
+
+        def fetch(into, t, offsets, h, sign=1.0):
+            nc.scalar.activation(into, listed(t, offsets, h * HALF, (h + 1) * HALF), COPY, scale=sign)
+            return into
+
+        steps = {}
+
+        def turn(k, slot, width, bank, fetched, first):
+            if k not in steps:
+                steps.setdefault(k, psum.tile([P, width], F32, name=f"step{k}", tag=f"bank{bank}"))
+            nc.tensor.matmul(
+                steps[k][:, slot * P : (slot + 1) * P], fetched[:, (k % 2) * P : (k % 2 + 1) * P], identity[:],
+                start=first, stop=not first, is_transpose=True,
+            )
+
+        frac_cols = keep.tile([P, T // P], F32, name="frac_cols")
+
+        def scale_and_return(k, width, home, scaled=None):
+            if scaled is None:
+                scaled = keep.tile([P, width], F32, name=f"scaled{k}")[:]
+            nc.scalar.activation(scaled, steps[k][:], COPY, scale=frac_cols[:, k : k + 1])
+            for slot in range(width // P):
+                nc.tensor.transpose(home[:, slot, (k % 2) * P : (k % 2 + 1) * P], scaled[:, slot * P : (slot + 1) * P], identity[:])
+            return scaled
 
         def weigh(terms, fetched, weight, t0, t1, a, b):
             spread = weight[:, a:b].unsqueeze(1).to_broadcast([P, t1 - t0, b - a])
@@ -138,13 +175,19 @@ def tile_picked_wlerp_none_lo_kernel(
         def store(t0, t1, a, b):
             nc.sync.dma_start(out=out_rows[:, t0:t1, a:b], in_=whole[:, t0:t1, a:b])
 
-        def quantise_out(h):
-            cols = slice(h * HALF, (h + 1) * HALF)
-            nc.vector.quantize_mx(out=o_codes[:, cols].bitcast(FP8X4), scales=o_plane[:, cols], in_=rounded[h][:])
-            nc.sync.dma_start(out=out_words[:, cols], in_=o_codes[:, cols].bitcast(I32))
+        def quantise_out(a, b):
+            h = a // HALF
+            nc.vector.quantize_mx(
+                out=o_codes[:, a:b].bitcast(FP8X4),
+                scales=o_plane[:, a:b],
+                in_=rounded[h][:, PACK * (a - h * HALF) : PACK * (b - h * HALF)],
+            )
 
-        def project(t):
-            nc.scalar.copy(out=y[t][:], in_=product(t, 0, T, 1 + t)[:])
+        def store_codes(a, b):
+            nc.sync.dma_start(out=out_words[:, a:b], in_=o_codes[:, a:b].bitcast(I32))
+
+        def project(t, a, b, bank):
+            nc.scalar.copy(out=y[t][:, a:b], in_=product(t, a, b, bank)[:])
 
         deal(nc.vector.tensor_copy, 0, 0, 40)
         deal(nc.scalar.copy, 0, 40, 64)
@@ -160,47 +203,69 @@ def tile_picked_wlerp_none_lo_kernel(
         nc.scalar.copy(out=y[0][:, 0:HALF], in_=acc[:])
         acc = product(0, HALF, T, 1)
         nc.vector.tensor_copy(out=y[0][:, HALF:T], in_=acc[:])
-        fetch_left(0, 0, HALF)
-        fetch_left(0, HALF, T)
-        far(0, 0, HALF)
+        left0 = fetch(lefts[:, 0, 0:HALF], 0, left_sb, 0, -1.0)
+        near_fused(0, HALF, T)
         far(0, HALF, T)
-        project(1)
-        project(2)
-        near(0, 1, 0, T)
-        far(1, 0, HALF)
-        add(0, 1, 0, T)
-        store(0, 1, 0, T)
-        fetch_left(1, 0, HALF)
-        fetch_left(1, HALF, T)
-        far(2, 0, HALF)
-        near(1, 2, 0, T)
-        project(3)
-        fetch_right(1, HALF, T)
-        far(3, 0, HALF)
-        weigh(fars, rights, frac_sb, 1, 2, HALF, T)
-        fetch_left(2, 0, HALF)
-        fetch_left(3, 0, HALF)
-        far(3, HALF, T)
+        project(1, 0, HALF, 2)
+        project(1, HALF, T, 3)
+        project(2, 0, T, 4)
+        acc3 = product(3, 0, T, 4)
+        right0 = fetch(rights[:, 0, 0:HALF], 0, right_sb, 0)
+        spread = psum.tile([P, T // P, P], F32, name="spread", tag="bank6")
+        for k in range(T // P):
+            nc.tensor.transpose(spread[:, k, :], frac_sb[:, k * P : (k + 1) * P], identity[:])
+        nc.scalar.copy(out=frac_cols[:], in_=spread[:, :, 0])
+        for fetched, first in ((left0, True), (right0, False)):
+            for k in range(2):
+                turn(k, 0, HALF, k, fetched, first)
+        far(1, 0, T)
+        near_fused(1, 0, T)
+        add(0, 1, HALF, T)
+        left2 = fetch(lefts[:, 2, 0:HALF], 2, left_sb, 0, -1.0)
+        right2 = fetch(laid.tile([P, HALF], F32, name="right2a", offset=512)[:], 2, right_sb, 0)
+        for fetched, first in ((left2, True), (right2, False)):
+            for k in range(2):
+                turn(k, 1, HALF, k, fetched, first)
+        nc.scalar.copy(out=y[3][:], in_=acc3[:])
         add(1, 2, 0, T)
-        store(1, 2, 0, T)
-        near(2, 4, 0, HALF)
-        fetch_right(2, HALF, T)
-        fetch_left(2, HALF, T)
-        fetch_left(3, HALF, T)
-        weigh(fars, rights, frac_sb, 2, 3, HALF, T)
-        add(2, 4, 0, HALF)
-        store(2, 4, 0, HALF)
+        flat_out = out_rows.rearrange("p t v -> p (t v)")
+        flat = whole[:].rearrange("p t v -> p (t v)")
+        nc.sync.dma_start(out=flat_out[:, HALF : 2 * T], in_=flat[:, HALF : 2 * T])
+        home0 = psum.tile([P, 2, HALF], F32, name="home0", tag="bank2")
+        spent = scale_and_return(0, HALF, home0)
+        scale_and_return(1, HALF, home0, whole[:, 3, 64 : 64 + HALF])
+        far(3, 0, HALF)
+        near_fused(3, 0, HALF)
+        left2 = fetch(laid.tile([P, HALF], F32, name="left2b", offset=0)[:], 2, left_sb, 1, -1.0)
+        right2 = fetch(laid.tile([P, HALF], F32, name="right2b", offset=1024)[:], 2, right_sb, 1)
+        for fetched, first in ((left2, True), (right2, False)):
+            for k in range(2, 4):
+                turn(k, 0, P, 3 if k == 2 else 5, fetched, first)
+        nc.vector.tensor_tensor(whole[:, 0:3:2, 0:HALF], home0[:], lefts[:, 0:3:2, 0:HALF], SUB)
+        nc.sync.dma_start(out=out_rows[:, 0:3:2, 0:HALF], in_=whole[:, 0:3:2, 0:HALF])
+        add(3, 4, 0, HALF)
+        nc.vector.tensor_tensor(whole[:, 3, HALF:T], listed(3, right_sb, HALF, T), frac_sb[:, HALF:T], MULT)
+        left3 = fetch(spent, 3, left_sb, 1)
+        home1 = psum.tile([P, 1, HALF], F32, name="home1", tag="bank7")
+        for k in range(2, 4):
+            scale_and_return(k, P, home1)
         nc.scalar.copy(*weave(0, HALF))
-        near(2, 4, HALF, 3 * P)
-        near(2, 4, 3 * P, T)
-        add(2, 4, HALF, 3 * P)
-        add(2, 4, 3 * P, T)
-        store(2, 4, HALF, T)
-        nc.scalar.copy(*weave(HALF, HALF + 96))
-        quantise_out(0)
-        nc.vector.tensor_copy(*weave(HALF + 96, 3 * P))
+        for k in (2, 3):
+            cols = slice(k * P, (k + 1) * P)
+            nc.vector.tensor_tensor(nears[:, 3, cols], left3[:, (k - 2) * P : (k - 1) * P], rest_sb[:, cols], MULT)
+        for k in (2, 3):
+            cols = slice(k * P, (k + 1) * P)
+            nc.vector.tensor_tensor(whole[:, 3, cols], nears[:, 3, cols], whole[:, 3, cols], ADD)
+        store(3, 4, 0, T)
+        nc.vector.tensor_tensor(whole[:, 2:3, HALF:T], home1[:], left2.unsqueeze(1), SUB)
+        store(2, 3, HALF, T)
+        nc.scalar.copy(*weave(HALF, 3 * P))
+        quantise_out(0, HALF)
+        store_codes(0, HALF)
         nc.vector.tensor_copy(*weave(3 * P, T))
-        quantise_out(1)
+        quantise_out(HALF, 3 * P)
+        quantise_out(3 * P, T)
+        store_codes(HALF, T)
         for q in range(4):
             engine = nc.sync if q % 2 == 0 else nc.scalar
             engine.dma_start(

from contextlib import ExitStack

import concourse.mybir as mybir
from concourse.masks import make_identity

K, T, N = 512, 512, 512
FLOPS = 2 * K * T * N

F32 = mybir.dt.float32
BF16 = mybir.dt.bfloat16
I32 = mybir.dt.int32
U32 = mybir.dt.uint32
U16 = mybir.dt.uint16
U8 = mybir.dt.uint8
FP8X4 = mybir.dt.float8_e4m3fn_x4
MULT = mybir.AluOpType.mult
ADD = mybir.AluOpType.add
SUB = mybir.AluOpType.subtract
COPY = mybir.ActivationFunctionType.Copy

P = 128
PACK = 4
LIST_ROWS = 16
HALF = T // 2
SPARE = 16
PIECES = [(0, 64), (64, 128)]


def tile_picked_wlerp_none_lo_kernel(
    tc, x_words, x_scales, w1, frac, left, right, out_0, out_1, out_2
):
    nc = tc.nc
    with ExitStack() as ctx:
        keep = ctx.enter_context(tc.tile_pool(name="keep", bufs=1))
        laid = ctx.enter_context(tc.tile_pool(name="laid", bufs=1))
        psum = ctx.enter_context(tc.psum_pool(name="psum", bufs=1))

        left_sb = keep.tile([P, T // LIST_ROWS], U16, name="left_sb")
        right_sb = keep.tile([P, T // LIST_ROWS], U16, name="right_sb")
        x_codes = keep.tile([P, T], U32, name="x_codes", align_bytes=64)
        x_plane = keep.tile([P, T], U8, name="x_plane", align_bytes=64)
        frac_sb = keep.tile([P, T], F32, name="frac_sb")
        rest_sb = keep.tile([P, T], F32, name="rest_sb")
        identity = keep.tile([P, P], F32, name="identity")
        nc.vector.memset(x_plane[:].bitcast(I32), 0)
        make_identity(nc, identity[:])

        w_rows = w1.rearrange("(p j) m -> p j m", j=PACK)
        w_raw = [keep.tile([P, PACK, PACK * (b - a)], F32, name=f"w_raw{c}") for c, (a, b) in enumerate(PIECES)]

        def load_w(c):
            a, b = PIECES[c]
            nc.sync.dma_start(out=w_raw[c][:], in_=w_rows[:, :, PACK * a : PACK * b])

        def load_scales(q, engine):
            engine.dma_start(
                out=x_plane[32 * q : 32 * q + 4, :].bitcast(I32),
                in_=x_scales[0, 4 * q : 4 * q + 4, :].bitcast(I32),
            )

        nc.sync.dma_start(left_sb[:], left)
        load_w(0)
        load_w(1)
        nc.sync.dma_start(
            out=x_codes[:].bitcast(I32),
            in_=x_words[0].rearrange("p c r -> p (c r)").bitcast(I32),
        )
        for q in range(4):
            load_scales(q, nc.sync)
        nc.sync.dma_start(out=frac_sb[:], in_=frac)
        nc.sync.dma_start(right_sb[:], right)

        w_dealt = [keep.tile([P, PACK * 64 * PACK], BF16, name=f"w_dealt{u}", align_bytes=64) for u in range(2)]
        w_codes = [keep.tile([P, P], U32, name=f"w_codes{t}", align_bytes=64) for t in range(PACK)]
        w_plane = [keep.tile([P, P], U8, name=f"w_plane{t}", align_bytes=64) for t in range(PACK)]
        y = [keep.tile([P, T + SPARE if t == 1 else T], F32, name=f"y{t}") for t in range(PACK)]
        nc.gpsimd.memset(y[1][:, T:], 0.0)

        def deal(copy, c, q0, q1):
            a = PIECES[c][0]
            u = a // 64
            source = w_raw[c][:].rearrange("p j (q t) -> p q j t", t=PACK)
            dealt = w_dealt[u][:].rearrange("p (t q j) -> p q j t", t=PACK, j=PACK)
            copy(dealt[:, q0 - 64 * u : q1 - 64 * u], source[:, q0 - a : q1 - a])

        def quantise_w(u, t):
            nc.vector.quantize_mx(
                out=w_codes[t][:, 64 * u : 64 * u + 64].bitcast(FP8X4),
                scales=w_plane[t][:, 64 * u : 64 * u + 64],
                in_=w_dealt[u][:, t * 256 : (t + 1) * 256],
            )

        def product(t, a, b, bank):
            acc = psum.tile([P, b - a], F32, name=f"acc{t}_{a}", tag=f"bank{bank}")
            nc.tensor.matmul_mx(
                out=acc[:],
                lhsT=w_codes[t][:].bitcast(FP8X4),
                lhsT_scale=w_plane[t][:],
                rhs=x_codes[:, a:b].bitcast(FP8X4),
                rhs_scale=x_plane[:, a:b],
                start=True,
                stop=True,
            )
            return acc

        out_rows = out_0.rearrange("(p t) v -> p t v", t=PACK)
        out_words = out_1[0].rearrange("p c r -> p (c r)").bitcast(I32)
        o_plane = keep.tile([P, T], U8, name="o_plane", align_bytes=64)
        o_codes = keep.tile([P, T], U32, name="o_codes", align_bytes=64)
        whole = keep.tile([P, PACK, T], F32, name="whole")
        lefts = keep.tile([P, PACK, T], F32, name="lefts")
        nears = keep.tile([P, PACK, T], F32, name="nears")
        rights = keep.tile([P, PACK, T], F32, name="rights")
        fars = keep.tile([P, PACK, T], F32, name="fars")
        rounded = [
            laid.tile([P, PACK * HALF], BF16, name="rounded0", align_bytes=64, offset=1536),
            keep.tile([P, PACK * HALF], BF16, name="rounded1", align_bytes=64),
        ]

        def listed(t, offsets, a, b):
            return y[t][:].indirect(offsets[:, a // LIST_ROWS : b // LIST_ROWS])

        def fetch_left(t, a, b):
            nc.scalar.activation(lefts[:, t, a:b], listed(t, left_sb, a, b), COPY)

        def fetch_right(t, a, b):
            nc.scalar.activation(rights[:, t, a:b], listed(t, right_sb, a, b), COPY)

        def far(t, a, b):
            nc.vector.tensor_tensor(fars[:, t, a:b], listed(t, right_sb, a, b), frac_sb[:, a:b], MULT)

        def near_fused(t, a, b):
            nc.vector.tensor_tensor(nears[:, t, a:b], listed(t, left_sb, a, b), rest_sb[:, a:b], MULT)

        def fetch(into, t, offsets, h, sign=1.0):
            nc.scalar.activation(into, listed(t, offsets, h * HALF, (h + 1) * HALF), COPY, scale=sign)
            return into

        steps = {}

        def turn(k, slot, width, bank, fetched, first):
            if k not in steps:
                steps.setdefault(k, psum.tile([P, width], F32, name=f"step{k}", tag=f"bank{bank}"))
            nc.tensor.matmul(
                steps[k][:, slot * P : (slot + 1) * P], fetched[:, (k % 2) * P : (k % 2 + 1) * P], identity[:],
                start=first, stop=not first, is_transpose=True,
            )

        frac_cols = keep.tile([P, T // P], F32, name="frac_cols")

        def scale_and_return(k, width, home, scaled=None):
            if scaled is None:
                scaled = keep.tile([P, width], F32, name=f"scaled{k}")[:]
            nc.scalar.activation(scaled, steps[k][:], COPY, scale=frac_cols[:, k : k + 1])
            for slot in range(width // P):
                nc.tensor.transpose(home[:, slot, (k % 2) * P : (k % 2 + 1) * P], scaled[:, slot * P : (slot + 1) * P], identity[:])
            return scaled

        def weigh(terms, fetched, weight, t0, t1, a, b):
            spread = weight[:, a:b].unsqueeze(1).to_broadcast([P, t1 - t0, b - a])
            nc.vector.tensor_tensor(terms[:, t0:t1, a:b], fetched[:, t0:t1, a:b], spread, MULT)

        def near(t0, t1, a, b):
            weigh(nears, lefts, rest_sb, t0, t1, a, b)

        def add(t0, t1, a, b):
            nc.vector.tensor_tensor(whole[:, t0:t1, a:b], nears[:, t0:t1, a:b], fars[:, t0:t1, a:b], ADD)

        def weave(a, b):
            h = a // HALF
            woven = rounded[h][:, PACK * (a - h * HALF) : PACK * (b - h * HALF)]
            source = whole[:, :, a:b].rearrange("p t (c i) -> p c t i", i=PACK)
            return woven.rearrange("p (c i t) -> p c t i", i=PACK, t=PACK), source

        def store(t0, t1, a, b):
            nc.sync.dma_start(out=out_rows[:, t0:t1, a:b], in_=whole[:, t0:t1, a:b])

        def quantise_out(a, b):
            h = a // HALF
            nc.vector.quantize_mx(
                out=o_codes[:, a:b].bitcast(FP8X4),
                scales=o_plane[:, a:b],
                in_=rounded[h][:, PACK * (a - h * HALF) : PACK * (b - h * HALF)],
            )

        def store_codes(a, b):
            nc.sync.dma_start(out=out_words[:, a:b], in_=o_codes[:, a:b].bitcast(I32))

        def project(t, a, b, bank):
            nc.scalar.copy(out=y[t][:, a:b], in_=product(t, a, b, bank)[:])

        deal(nc.vector.tensor_copy, 0, 0, 40)
        deal(nc.scalar.copy, 0, 40, 64)
        for t in range(PACK):
            quantise_w(0, t)
        deal(nc.vector.tensor_copy, 1, 64, 102)
        deal(nc.scalar.copy, 1, 102, 128)
        for t in range(PACK):
            quantise_w(1, t)
        nc.vector.tensor_scalar(rest_sb[:], frac_sb[:], -1.0, 1.0, MULT, ADD)

        acc = product(0, 0, HALF, 0)
        nc.scalar.copy(out=y[0][:, 0:HALF], in_=acc[:])
        acc = product(0, HALF, T, 1)
        nc.vector.tensor_copy(out=y[0][:, HALF:T], in_=acc[:])
        left0 = fetch(lefts[:, 0, 0:HALF], 0, left_sb, 0, -1.0)
        near_fused(0, HALF, T)
        far(0, HALF, T)
        project(1, 0, HALF, 2)
        project(1, HALF, T, 3)
        project(2, 0, T, 4)
        acc3 = product(3, 0, T, 4)
        right0 = fetch(rights[:, 0, 0:HALF], 0, right_sb, 0)
        spread = psum.tile([P, T // P, P], F32, name="spread", tag="bank6")
        for k in range(T // P):
            nc.tensor.transpose(spread[:, k, :], frac_sb[:, k * P : (k + 1) * P], identity[:])
        nc.scalar.copy(out=frac_cols[:], in_=spread[:, :, 0])
        for fetched, first in ((left0, True), (right0, False)):
            for k in range(2):
                turn(k, 0, HALF, k, fetched, first)
        far(1, 0, T)
        near_fused(1, 0, T)
        add(0, 1, HALF, T)
        left2 = fetch(lefts[:, 2, 0:HALF], 2, left_sb, 0, -1.0)
        right2 = fetch(laid.tile([P, HALF], F32, name="right2a", offset=512)[:], 2, right_sb, 0)
        for fetched, first in ((left2, True), (right2, False)):
            for k in range(2):
                turn(k, 1, HALF, k, fetched, first)
        nc.scalar.copy(out=y[3][:], in_=acc3[:])
        add(1, 2, 0, T)
        flat_out = out_rows.rearrange("p t v -> p (t v)")
        flat = whole[:].rearrange("p t v -> p (t v)")
        nc.sync.dma_start(out=flat_out[:, HALF : 2 * T], in_=flat[:, HALF : 2 * T])
        home0 = psum.tile([P, 2, HALF], F32, name="home0", tag="bank2")
        spent = scale_and_return(0, HALF, home0)
        scale_and_return(1, HALF, home0, whole[:, 3, 64 : 64 + HALF])
        far(3, 0, HALF)
        near_fused(3, 0, HALF)
        left2 = fetch(laid.tile([P, HALF], F32, name="left2b", offset=0)[:], 2, left_sb, 1, -1.0)
        right2 = fetch(laid.tile([P, HALF], F32, name="right2b", offset=1024)[:], 2, right_sb, 1)
        for fetched, first in ((left2, True), (right2, False)):
            for k in range(2, 4):
                turn(k, 0, P, 3 if k == 2 else 5, fetched, first)
        nc.vector.tensor_tensor(whole[:, 0:3:2, 0:HALF], home0[:], lefts[:, 0:3:2, 0:HALF], SUB)
        nc.sync.dma_start(out=out_rows[:, 0:3:2, 0:HALF], in_=whole[:, 0:3:2, 0:HALF])
        add(3, 4, 0, HALF)
        nc.vector.tensor_tensor(whole[:, 3, HALF:T], listed(3, right_sb, HALF, T), frac_sb[:, HALF:T], MULT)
        left3 = fetch(spent, 3, left_sb, 1)
        home1 = psum.tile([P, 1, HALF], F32, name="home1", tag="bank7")
        for k in range(2, 4):
            scale_and_return(k, P, home1)
        nc.scalar.copy(*weave(0, HALF))
        for k in (2, 3):
            cols = slice(k * P, (k + 1) * P)
            nc.vector.tensor_tensor(nears[:, 3, cols], left3[:, (k - 2) * P : (k - 1) * P], rest_sb[:, cols], MULT)
        for k in (2, 3):
            cols = slice(k * P, (k + 1) * P)
            nc.vector.tensor_tensor(whole[:, 3, cols], nears[:, 3, cols], whole[:, 3, cols], ADD)
        store(3, 4, 0, T)
        nc.vector.tensor_tensor(whole[:, 2:3, HALF:T], home1[:], left2.unsqueeze(1), SUB)
        store(2, 3, HALF, T)
        nc.scalar.copy(*weave(HALF, 3 * P))
        quantise_out(0, HALF)
        store_codes(0, HALF)
        nc.vector.tensor_copy(*weave(3 * P, T))
        quantise_out(HALF, 3 * P)
        quantise_out(3 * P, T)
        store_codes(HALF, T)
        for q in range(4):
            engine = nc.sync if q % 2 == 0 else nc.scalar
            engine.dma_start(
                out=out_2[0, 4 * q : 4 * q + 4, :].bitcast(I32),
                in_=o_plane[32 * q : 32 * q + 4, :].bitcast(I32),
            )
